import numpy as np
import ml_dtypes


def mxq(x, axis, fmt="e4m3"):
    dtype, down = {"e4m3": (ml_dtypes.float8_e4m3fn, 7), "e5m2": (ml_dtypes.float8_e5m2, 14)}[fmt]
    v = np.moveaxis(np.asarray(x, np.float32).astype(ml_dtypes.bfloat16).astype(np.float64), axis, -1)
    blocks = v.reshape(v.shape[:-1] + (-1, 32))
    amax = np.abs(blocks).max(-1, keepdims=True)
    byte = np.maximum(np.where(amax > 0, np.frexp(amax)[1] - 1 + 127, 0) - down, 1)
    scale = np.exp2(byte - 127.0)
    codes = (blocks / scale).astype(np.float32).astype(dtype).astype(np.float64)
    return np.moveaxis((codes * scale).reshape(v.shape), -1, axis)


WIDE = False


def mx_kscale(k):
    if not WIDE:
        return np.ones(k)
    levels = np.array([10, -10, 5, -5, 0])
    if k % 512:
        return np.exp2(np.random.permutation(np.resize(levels, k // 32))).repeat(32)
    a = np.empty((k // 512, 16))
    for p in range(k // 512):
        a[p, :8] = np.random.permutation(np.resize(levels, 8))
        for g in range(8):
            far = levels[np.abs(levels - a[p, g]) >= 10]
            a[p, g + 8] = far[np.random.randint(len(far))]
    return np.exp2(a.ravel()).repeat(32)


def f64(x):
    return np.asarray(x).astype(np.float64)


def striped(idx):
    return np.tile(idx.reshape(-1, 16).T, (8, 1)).astype(np.uint16)


def unstriped(offs):
    return offs[:16].T.reshape(-1).astype(np.int64)


E2M1 = np.array([0.0, 0.5, 1.0, 1.5, 2.0, 3.0, 4.0, 6.0, -0.0, -0.5, -1.0, -1.5, -2.0, -3.0, -4.0, -6.0])


def pack_weight(w, fmt):
    k, n = w.shape
    w = f64(np.asarray(w, np.float32).astype(ml_dtypes.bfloat16)).reshape(k // 32, 32, n)
    amax = np.abs(w).max(1)
    if fmt == "e4m3":
        byte = np.frexp(amax)[1] - 1 + 127 - 7
    else:
        mant, ex = np.frexp(amax / 6.0)
        byte = np.where(mant > 0.5, ex, ex - 1) + 127
    byte = np.clip(np.where(amax > 0, byte, 1), 1, 254)
    scaled = (w * np.exp2(127.0 - byte)[:, None, :]).reshape(k, n).astype(np.float32)
    by_word = np.ascontiguousarray(scaled.reshape(k // 512, 128, 4, n).transpose(0, 1, 3, 2))
    if fmt == "e4m3":
        words = by_word.astype(ml_dtypes.float8_e4m3fn).view(np.uint8)
    else:
        c = by_word.astype(ml_dtypes.float4_e2m1fn).view(np.uint8) & 0xF
        words = (c[..., 0::2] | (c[..., 1::2] << 4)).reshape(k // 512, 128, 2 * n)
    return np.ascontiguousarray(words), np.ascontiguousarray(byte.astype(np.uint8).reshape(k // 512, 16, n))


def unpack_weight(words, scales, fmt):
    g, _, n = scales.shape
    words = np.ascontiguousarray(words).reshape(g, 128, n, -1)
    if fmt == "e4m3":
        vals = words.view(ml_dtypes.float8_e4m3fn).astype(np.float64)
    else:
        nib = np.empty((g, 128, n, 4), np.uint8)
        nib[..., 0::2] = words & 0xF
        nib[..., 1::2] = words >> 4
        vals = E2M1[nib]
    vals = vals * np.repeat(np.exp2(scales.astype(np.float64) - 127.0), 8, axis=1)[..., None]
    return vals.transpose(0, 1, 3, 2).reshape(g * 512, n)


def relu(v):
    return np.maximum(v, 0.0)


K, T, E, C, H, HS, N = 1024, 512, 12, 128, 512, 512, 128
TOP = 3


def by_expert(wq, xq):
    return np.concatenate([wq[e].T @ xq[:, e * C:(e + 1) * C] for e in range(E)], axis=1)


def setup_inputs():
    n = np.random.standard_normal
    s = mx_kscale(K)
    u = mx_kscale(H)
    v = mx_kscale(HS)
    deal = np.repeat(np.arange(E), C).reshape(TOP, T)[:, np.random.permutation(T)]
    deal = np.take_along_axis(deal, np.argsort(np.random.rand(TOP, T), axis=0), axis=0)
    for _ in range(8):
        s_, t_ = np.random.permutation(T).reshape(2, -1); r = np.random.randint(TOP, size=T // 2); x, y = deal[r, s_].copy(), deal[r, t_].copy()
        ok = ~((deal[:, s_] == y).any(0) | (deal[:, t_] == x).any(0)); deal[r[ok], s_[ok]] = y[ok]; deal[r[ok], t_[ok]] = x[ok]
    order = np.lexsort((np.random.rand(TOP * T), deal.reshape(-1)))
    slot_token = order % T; pos = np.empty(TOP * T, np.int64); pos[order] = np.arange(TOP * T); pos = pos.reshape(TOP, T)
    g = np.random.uniform(0.5, 1.5, (TOP, T)); g = g / g.sum(0)
    x = pack_weight(n((K, T)) * s[:, None], "e4m3")
    w1 = [pack_weight(m, "e2m1") for m in n((E, K, H)) / np.sqrt(K) / s[None, :, None] * u]
    w2 = [pack_weight(m, "e2m1") for m in n((E, H, N)) / np.sqrt(H) / u[None, :, None]]
    w1s = pack_weight(n((K, HS)) / np.sqrt(K) / s[:, None] * v, "e4m3")
    w2s = pack_weight(n((HS, N)) / np.sqrt(HS) / v[:, None], "e4m3")
    return {
        "x_words": x[0],
        "x_scales": x[1],
        "w1_words": np.stack([m[0] for m in w1]),
        "w1_scales": np.stack([m[1] for m in w1]),
        "w2_words": np.stack([m[0] for m in w2]),
        "w2_scales": np.stack([m[1] for m in w2]),
        "w1s_words": w1s[0],
        "w1s_scales": w1s[1],
        "w2s_words": w2s[0],
        "w2s_scales": w2s[1],
        "gate": np.stack([np.tile(r, (128, 1)) for r in g]).astype(np.float32),
        "offs": striped(slot_token),
        "pos1": striped(pos[0]),
        "pos2": striped(pos[1]),
        "pos3": striped(pos[2]),
    }


def reference(x_words, x_scales, w1_words, w1_scales, w2_words, w2_scales, w1s_words, w1s_scales, w2s_words, w2s_scales, gate, offs, pos1, pos2, pos3):
    w1 = np.stack([unpack_weight(w1_words[e], w1_scales[e], "e2m1") for e in range(E)])
    w2 = np.stack([unpack_weight(w2_words[e], w2_scales[e], "e2m1") for e in range(E)])
    w1s = unpack_weight(w1s_words, w1s_scales, "e4m3")
    w2s = unpack_weight(w2s_words, w2s_scales, "e4m3")
    idx = unstriped(offs)
    x = unpack_weight(x_words, x_scales, "e4m3")
    hs = relu(w1s.T @ x)
    ys = w2s.T @ mxq(hs, 0, "e4m3")
    h = relu(by_expert(w1, x[:, idx]))
    y = by_expert(w2, mxq(h, 0, "e4m3"))
    c = sum(f64(gate[r, :1]) * y[:, unstriped(p)] for r, p in enumerate((pos1, pos2, pos3)))
    return ys + c

@@ -1,0 +1,228 @@
+from contextlib import ExitStack
+
+import concourse.mybir as mybir
+from concourse.masks import make_identity
+
+K, T, E, C, H, N = 1024, 512, 12, 128, 512, 128
+TOP = 3
+P = 128
+PASSES = K // 512
+SLOTS = E * C
+FLOPS = 2 * (SLOTS + T) * (K * H + H * N)
+
+F32 = mybir.dt.float32
+BF16 = mybir.dt.bfloat16
+I32 = mybir.dt.int32
+U32 = mybir.dt.uint32
+U16 = mybir.dt.uint16
+U8 = mybir.dt.uint8
+FP8X4 = mybir.dt.float8_e4m3fn_x4
+FP4X4 = mybir.dt.float4_e2m1fn_x4
+RELU = mybir.ActivationFunctionType.Relu
+MULT = mybir.AluOpType.mult
+ADD = mybir.AluOpType.add
+
+GROUPS = [[0], [1, 2], [3, 4], [5, 6], [7, 8], [9, 10], [11]]
+EARLY = 5
+
+
+def load_scale_rows(queue, plane, rows):
+    blocks = rows.shape[0]
+    src = rows.bitcast(I32).rearrange("b (q r) w -> r q b w", r=4)
+    dst = plane.bitcast(I32).rearrange("p (b w) -> p b w", b=blocks)
+    for r in range(4):
+        queue.dma_start(out=dst[r:P:32], in_=src[r])
+
+
+def tile_moe_shf_mlp_relu_kernel(
+    tc, x_words, x_scales, w1_words, w1_scales, w2_words, w2_scales, w1s_words, w1s_scales, w2s_words, w2s_scales,
+    gate, offs, pos1, pos2, pos3, out,
+):
+    nc = tc.nc
+    with ExitStack() as ctx:
+        keep = ctx.enter_context(tc.tile_pool(name="keep", bufs=1))
+        psum = ctx.enter_context(tc.psum_pool(name="psum", bufs=1))
+
+        def sb(name, shape, dtype):
+            return keep.tile(shape, dtype, name=name, align_bytes=64)
+
+        offs_sb = keep.tile([P, SLOTS // 16], U16, name="offs_sb")
+        pos_sb = [keep.tile([P, T // 16], U16, name="pos%d_sb" % r) for r in range(TOP)]
+        xw = [sb("xw%d" % s, [P, T], I32) for s in range(PASSES)]
+        xs = sb("xs", [P, PASSES * T], U8)
+        w1sc_a = sb("w1sc_a", [P, EARLY * PASSES * H], U8)
+        w1sc_b = sb("w1sc_b", [P, (E - EARLY) * PASSES * H], U8)
+        w2sc = sb("w2sc", [P, E * N], U8)
+        w1ssc = sb("w1ssc", [P, PASSES * H], U8)
+        w2ssc = sb("w2ssc", [P, N], U8)
+        w1 = [sb("w1_%d" % g, [P, len(es) * PASSES, 2 * H], U8) for g, es in enumerate(GROUPS)]
+        w2 = sb("w2", [P, E, 2 * N], U8)
+        w1s = sb("w1s", [P, PASSES, H], I32)
+        w2s = sb("w2s", [P, N], I32)
+        gates = sb("gates", [P, TOP, T], F32)
+        ident = sb("ident", [P, P], F32)
+        warm = sb("warm", [P, 1], F32)
+        y_slots = sb("y_slots", [P, SLOTS], F32)
+
+        def load_w1(g):
+            es = GROUPS[g]
+            src = w1_words[es[0]:es[-1] + 1].bitcast(I32).rearrange("e s p c -> p (e s) c")
+            nc.sync.dma_start(out=w1[g][:].bitcast(I32), in_=src)
+
+        def x_pass(s):
+            return x_words[s].rearrange("p t d -> p (t d)").bitcast(I32)
+
+        for plane in (xs, w1sc_a, w2sc, w1sc_b, w1ssc, w2ssc):
+            nc.vector.memset(plane[:].bitcast(I32), 0)
+        make_identity(nc, ident[:])
+
+        w1_rows = w1_scales.rearrange("e s b i -> (e s) b i")
+        nc.sync.dma_start(offs_sb[:], offs)
+        nc.sync.dma_start(out=xw[0][:], in_=x_pass(0))
+        load_scale_rows(nc.scalar, xs[:], x_scales)
+        nc.sync.dma_start(out=xw[1][:], in_=x_pass(1))
+        load_scale_rows(nc.scalar, w1sc_a[:], w1_rows[:EARLY * PASSES])
+        nc.scalar.activation(warm[:], ident[:, 0:1], RELU)
+        load_w1(0)
+        load_w1(1)
+        load_scale_rows(nc.sync, w2sc[:], w2_scales.rearrange("e s b n -> (e s) b n"))
+        nc.sync.dma_start(out=w2[:].bitcast(I32), in_=w2_words.bitcast(I32).rearrange("e s p c -> p (e s) c"))
+        load_w1(2)
+        load_scale_rows(nc.sync, w1sc_b[:], w1_rows[EARLY * PASSES:])
+        load_w1(3)
+        nc.sync.dma_start(out=w1s[:], in_=w1s_words.rearrange("s p l d -> p s (l d)").bitcast(I32))
+        load_scale_rows(nc.sync, w1ssc[:], w1s_scales)
+        load_w1(4)
+        load_w1(5)
+        load_w1(6)
+        load_scale_rows(nc.sync, w2ssc[:], w2s_scales)
+        nc.sync.dma_start(out=w2s[:], in_=w2s_words[0].rearrange("p n d -> p (n d)").bitcast(I32))
+        for r, pos in enumerate((pos1, pos2, pos3)):
+            nc.sync.dma_start(pos_sb[r][:], pos)
+        nc.sync.dma_start(out=gates[:], in_=gate.rearrange("r p t -> p r t"))
+
+        gathered = {}
+        hidden = {}
+        grouped = {}
+        quantised = {}
+
+        def gather(g):
+            es = GROUPS[g]
+            n = len(es) * C
+            lst = offs_sb[:, es[0] * C // 16:(es[-1] + 1) * C // 16]
+            tiles = []
+            for s in range(PASSES):
+                words = sb("gw%d_%d" % (g, s), [P, n], U32)
+                scales = sb("gs%d_%d" % (g, s), [P, n], U8)
+                nc.vector.tensor_copy(words[:], xw[s][:].bitcast(U32).indirect(lst))
+                nc.vector.tensor_copy(scales[:], xs[:, s * T:(s + 1) * T].indirect(lst))
+                tiles.append((words, scales))
+            gathered[g] = tiles
+
+        def relu_out(key, u, bank):
+            h = sb("h%s_%d" % (key, u), [P, H], BF16)
+            nc.scalar.activation(
+                h[:].rearrange("p (v m d) -> p v m d", v=2, d=2),
+                bank[:].rearrange("p (m v d) -> p v m d", v=2, d=2), RELU)
+            hidden.setdefault(key, []).append(h)
+
+        def first_layer(g):
+            for u, e in enumerate(GROUPS[g]):
+                bank = psum.tile([P, H], F32, name="h_bank", bufs=4)
+                cols = slice(u * C, (u + 1) * C)
+                plane, first = (w1sc_a, e) if e < EARLY else (w1sc_b, e - EARLY)
+                for s in range(PASSES):
+                    words, scales = gathered[g][s]
+                    at = (first * PASSES + s) * H
+                    nc.tensor.matmul_mx(
+                        out=bank[:], lhsT=words[:, cols].bitcast(FP8X4), lhsT_scale=scales[:, cols],
+                        rhs=w1[g][:, u * PASSES + s, :].bitcast(FP4X4), rhs_scale=plane[:, at:at + H],
+                        start=(s == 0), stop=(s == PASSES - 1))
+                relu_out(g, u, bank)
+
+        def first_layer_shared(j):
+            for u in range(2):
+                bank = psum.tile([P, H], F32, name="h_bank", bufs=4)
+                t0 = (2 * j + u) * C
+                for s in range(PASSES):
+                    nc.tensor.matmul_mx(
+                        out=bank[:], lhsT=xw[s][:, t0:t0 + C].bitcast(FP8X4),
+                        lhsT_scale=xs[:, s * T + t0:s * T + t0 + C],
+                        rhs=w1s[:, s, :].bitcast(FP8X4), rhs_scale=w1ssc[:, s * H:(s + 1) * H],
+                        start=(s == 0), stop=(s == PASSES - 1))
+                relu_out("s%d" % j, u, bank)
+
+        def turn(key):
+            tiles = hidden[key]
+            n = len(tiles)
+            bank = psum.tile([P, 2, 2, C], F32, name="t_bank", bufs=2)
+            for u, h in enumerate(tiles):
+                pairs = h[:].bitcast(F32)
+                for v in range(2):
+                    nc.tensor.transpose(bank[:, u, v, :], pairs[:, v * P:(v + 1) * P], ident[:])
+            dst = sb("ht%s" % key, [P, n * C * 4], BF16)
+            nc.scalar.copy(
+                dst[:].bitcast(F32).rearrange("p (u j v) -> p u j v", u=n, v=2),
+                bank[:, 0:n].rearrange("p u v j -> p u j v"))
+            grouped[key] = dst
+
+        def quantise(key, codes, scales):
+            nc.vector.quantize_mx(out=codes.bitcast(FP8X4), scales=scales, in_=grouped[key][:])
+
+        def quantise_routed(g):
+            n = len(GROUPS[g]) * C
+            codes = sb("hq%d" % g, [P, n], U32)
+            scales = sb("hs%d" % g, [P, n], U8)
+            quantise(g, codes[:], scales[:])
+            quantised[g] = (codes, scales)
+
+        def second_layer(g):
+            es = GROUPS[g]
+            codes, scales = quantised[g]
+            bank = psum.tile([P, 2 * C], F32, name="y_bank", bufs=1)
+            for u, e in enumerate(es):
+                cols = slice(u * C, (u + 1) * C)
+                nc.tensor.matmul_mx(
+                    out=bank[:, cols], lhsT=w2[:, e, :].bitcast(FP4X4), lhsT_scale=w2sc[:, e * N:(e + 1) * N],
+                    rhs=codes[:, cols].bitcast(FP8X4), rhs_scale=scales[:, cols], start=True, stop=True)
+            nc.scalar.copy(y_slots[:, es[0] * C:(es[-1] + 1) * C], bank[:, 0:len(es) * C])
+
+        last = len(GROUPS) - 1
+        for i in range(last + 1):
+            gather(i)
+            if i >= 2:
+                quantise_routed(i - 2)
+            first_layer(i)
+            if i >= 2:
+                second_layer(i - 2)
+            turn(i)
+            if i in (3, 4):
+                first_layer_shared(i - 3)
+                turn("s%d" % (i - 3))
+        quantise_routed(last - 1)
+        second_layer(last - 1)
+        quantise_routed(last)
+        second_layer(last)
+
+        shared_codes = sb("sq", [P, T], U32)
+        shared_scales = sb("ss", [P, T], U8)
+        for j in range(2):
+            cols = slice(j * 2 * C, (j + 1) * 2 * C)
+            quantise("s%d" % j, shared_codes[:, cols], shared_scales[:, cols])
+        ys = psum.tile([P, T], F32, name="ys_bank")
+        nc.tensor.matmul_mx(
+            out=ys[:], lhsT=w2s[:].bitcast(FP8X4), lhsT_scale=w2ssc[:],
+            rhs=shared_codes[:].bitcast(FP8X4), rhs_scale=shared_scales[:], start=True, stop=True)
+
+        half = T // 2
+        for j in range(2):
+            cols = slice(j * half, (j + 1) * half)
+            terms = [sb("term%d_%d" % (j, r), [P, half], F32) for r in range(TOP)]
+            sums = [sb("sum%d_%d" % (j, r), [P, half], F32) for r in range(TOP)]
+            for r in range(TOP):
+                lst = pos_sb[r][:, j * half // 16:(j + 1) * half // 16]
+                nc.vector.tensor_tensor(terms[r][:], y_slots[:].indirect(lst), gates[:, r, cols], MULT)
+            nc.vector.tensor_tensor(sums[0][:], terms[0][:], ys[:, cols], ADD)
+            nc.vector.tensor_tensor(sums[1][:], terms[1][:], terms[2][:], ADD)
+            nc.vector.tensor_tensor(sums[2][:], sums[0][:], sums[1][:], ADD)
+            nc.sync.dma_start(out=out[:, cols], in_=sums[2][:])

@@ -22,8 +22,12 @@ RELU = mybir.ActivationFunctionType.Relu
 MULT = mybir.AluOpType.mult
 ADD = mybir.AluOpType.add
 
-GROUPS = [[0], [1, 2], [3, 4], [5, 6], [7, 8], [9, 10], [11]]
-EARLY = 5
+GROUPS = [[0, 1], [2, 3], [4, 5], [6, 7], [8, 9], [10, 11]]
+WORD_LOADS = [(0, 2), (2, 4), (4, 6), (6, 8), (8, 10), (10, 11), (11, 12)]
+HALF_E = E // 2
+HALF_SLOTS = SLOTS // 2
+PIECE = 384
+MOVED = 112
 
 
 def load_scale_rows(queue, plane, rows):
@@ -32,6 +36,11 @@ def load_scale_rows(queue, plane, rows):
     dst = plane.bitcast(I32).rearrange("p (b w) -> p b w", b=blocks)
     for r in range(4):
         queue.dma_start(out=dst[r:P:32], in_=src[r])
+
+
+def load_packed_scale_rows(queue, plane, rows):
+    for q in range(4):
+        queue.dma_start(out=plane.bitcast(I32)[32 * q:32 * q + 8, :], in_=rows.bitcast(I32)[:, 4 * q:4 * q + 4, :])
 
 
 def tile_moe_shf_mlp_relu_kernel(
@@ -49,121 +58,117 @@ def tile_moe_shf_mlp_relu_kernel(
         offs_sb = keep.tile([P, SLOTS // 16], U16, name="offs_sb")
         pos_sb = [keep.tile([P, T // 16], U16, name="pos%d_sb" % r) for r in range(TOP)]
         xw = [sb("xw%d" % s, [P, T], I32) for s in range(PASSES)]
-        xs = sb("xs", [P, PASSES * T], U8)
-        w1sc_a = sb("w1sc_a", [P, EARLY * PASSES * H], U8)
-        w1sc_b = sb("w1sc_b", [P, (E - EARLY) * PASSES * H], U8)
-        w2sc = sb("w2sc", [P, E * N], U8)
-        w1ssc = sb("w1ssc", [P, PASSES * H], U8)
-        w2ssc = sb("w2ssc", [P, N], U8)
-        w1 = [sb("w1_%d" % g, [P, len(es) * PASSES, 2 * H], U8) for g, es in enumerate(GROUPS)]
+        xs = sb("xs", [P, T], U8)
+        w1 = [sb("w1_%d" % lo, [P, (hi - lo) * PASSES, 2 * H], U8) for lo, hi in WORD_LOADS]
+        w1sc = [sb("w1sc_%d" % j, [P, HALF_E * PASSES * H], U8) for j in range(2)]
         w2 = sb("w2", [P, E, 2 * N], U8)
+        w2sc = sb("w2sc", [P, E * N], U8)
         w1s = sb("w1s", [P, PASSES, H], I32)
+        w1ssc = sb("w1ssc", [P, H], U8)
         w2s = sb("w2s", [P, N], I32)
-        gates = sb("gates", [P, TOP, T], F32)
+        w2ssc = sb("w2ssc", [P, N], U8)
+        gates = [sb("gate%d" % r, [P, T], F32) for r in range(TOP)]
         ident = sb("ident", [P, P], F32)
         warm = sb("warm", [P, 1], F32)
         y_slots = sb("y_slots", [P, SLOTS], F32)
+        slot_words = [sb("slot_words%d" % s, [P, SLOTS], U32) for s in range(PASSES)]
+        slot_scales = [sb("slot_scales%d" % j, [P, HALF_SLOTS], U8) for j in range(2)]
+        moved_scales = [sb("moved_scales%d" % j, [P, HALF_SLOTS], U8) for j in range(2)]
+        banks = [psum.tile([P, H], F32, name="bank%d" % b) for b in range(8)]
 
-        def load_w1(g):
-            es = GROUPS[g]
-            src = w1_words[es[0]:es[-1] + 1].bitcast(I32).rearrange("e s p c -> p (e s) c")
-            nc.sync.dma_start(out=w1[g][:].bitcast(I32), in_=src)
-
-        def x_pass(s):
-            return x_words[s].rearrange("p t d -> p (t d)").bitcast(I32)
-
-        for plane in (xs, w1sc_a, w2sc, w1sc_b, w1ssc, w2ssc):
+        for plane in (xs, w1ssc, w1sc[0]):
             nc.vector.memset(plane[:].bitcast(I32), 0)
         make_identity(nc, ident[:])
-
-        w1_rows = w1_scales.rearrange("e s b i -> (e s) b i")
-        nc.sync.dma_start(offs_sb[:], offs)
-        nc.sync.dma_start(out=xw[0][:], in_=x_pass(0))
-        load_scale_rows(nc.scalar, xs[:], x_scales)
-        nc.sync.dma_start(out=xw[1][:], in_=x_pass(1))
-        load_scale_rows(nc.scalar, w1sc_a[:], w1_rows[:EARLY * PASSES])
+        for plane in (w1sc[1], moved_scales[0], moved_scales[1], w2sc, w2ssc):
+            nc.gpsimd.memset(plane[:].bitcast(I32), 0)
         nc.scalar.activation(warm[:], ident[:, 0:1], RELU)
-        load_w1(0)
-        load_w1(1)
+
+        nc.sync.dma_start(offs_sb[:], offs)
+        load_packed_scale_rows(nc.sync, xs[:], x_scales)
+        load_packed_scale_rows(nc.sync, w1ssc[:], w1s_scales)
+        for s in range(PASSES):
+            nc.sync.dma_start(out=xw[s][:], in_=x_words[s].rearrange("p t d -> p (t d)").bitcast(I32))
+        nc.sync.dma_start(out=w1s[:], in_=w1s_words.rearrange("s p l d -> p s (l d)").bitcast(I32))
+        for j in range(2):
+            rows = w1_scales[j * HALF_E:(j + 1) * HALF_E].rearrange("e s b i -> (e s) b i")
+            load_scale_rows(nc.sync, w1sc[j][:], rows)
+        w1_of = {}
+        for tile, (lo, hi) in zip(w1, WORD_LOADS):
+            src = w1_words[lo:hi].bitcast(I32).rearrange("e s p c -> p (e s) c")
+            nc.sync.dma_start(out=tile[:].bitcast(I32), in_=src)
+            for e in range(lo, hi):
+                w1_of[e] = tile[:, (e - lo) * PASSES:(e - lo + 1) * PASSES, :]
         load_scale_rows(nc.sync, w2sc[:], w2_scales.rearrange("e s b n -> (e s) b n"))
         nc.sync.dma_start(out=w2[:].bitcast(I32), in_=w2_words.bitcast(I32).rearrange("e s p c -> p (e s) c"))
-        load_w1(2)
-        load_scale_rows(nc.sync, w1sc_b[:], w1_rows[EARLY * PASSES:])
-        load_w1(3)
-        nc.sync.dma_start(out=w1s[:], in_=w1s_words.rearrange("s p l d -> p s (l d)").bitcast(I32))
-        load_scale_rows(nc.sync, w1ssc[:], w1s_scales)
-        load_w1(4)
-        load_w1(5)
-        load_w1(6)
-        load_scale_rows(nc.sync, w2ssc[:], w2s_scales)
-        nc.sync.dma_start(out=w2s[:], in_=w2s_words[0].rearrange("p n d -> p (n d)").bitcast(I32))
         for r, pos in enumerate((pos1, pos2, pos3)):
             nc.sync.dma_start(pos_sb[r][:], pos)
-        nc.sync.dma_start(out=gates[:], in_=gate.rearrange("r p t -> p r t"))
+        for r in range(TOP):
+            nc.sync.dma_start(out=gates[r][:], in_=gate[r])
+        load_scale_rows(nc.sync, w2ssc[:], w2s_scales)
+        nc.sync.dma_start(out=w2s[:], in_=w2s_words[0].rearrange("p n d -> p (n d)").bitcast(I32))
 
-        gathered = {}
+        def slot_list(first, count):
+            return offs_sb[:, first // 16:(first + count) // 16]
+
+        for j in range(2):
+            for at in range(0, HALF_SLOTS, PIECE):
+                nc.vector.tensor_copy(slot_scales[j][:, at:at + PIECE],
+                                      xs[:].indirect(slot_list(j * HALF_SLOTS + at, PIECE)))
+            nc.scalar.dma_start(out=moved_scales[j][:].bitcast(I32)[0:MOVED, :],
+                                in_=slot_scales[j][:].bitcast(I32)[4:4 + MOVED, :])
+        for at in range(0, SLOTS, PIECE):
+            for s in range(PASSES):
+                nc.vector.tensor_copy(slot_words[s][:, at:at + PIECE],
+                                      xw[s][:].bitcast(U32).indirect(slot_list(at, PIECE)))
+
         hidden = {}
         grouped = {}
         quantised = {}
+        units = []
 
-        def gather(g):
-            es = GROUPS[g]
-            n = len(es) * C
-            lst = offs_sb[:, es[0] * C // 16:(es[-1] + 1) * C // 16]
-            tiles = []
-            for s in range(PASSES):
-                words = sb("gw%d_%d" % (g, s), [P, n], U32)
-                scales = sb("gs%d_%d" % (g, s), [P, n], U8)
-                nc.vector.tensor_copy(words[:], xw[s][:].bitcast(U32).indirect(lst))
-                nc.vector.tensor_copy(scales[:], xs[:, s * T:(s + 1) * T].indirect(lst))
-                tiles.append((words, scales))
-            gathered[g] = tiles
-
-        def relu_out(key, u, bank):
-            h = sb("h%s_%d" % (key, u), [P, H], BF16)
+        def relu_out(key, bank):
+            h = sb("h%d" % len(units), [P, H], BF16)
             nc.scalar.activation(
                 h[:].rearrange("p (v m d) -> p v m d", v=2, d=2),
                 bank[:].rearrange("p (m v d) -> p v m d", v=2, d=2), RELU)
             hidden.setdefault(key, []).append(h)
+            units.append(key)
 
         def first_layer(g):
-            for u, e in enumerate(GROUPS[g]):
-                bank = psum.tile([P, H], F32, name="h_bank", bufs=4)
-                cols = slice(u * C, (u + 1) * C)
-                plane, first = (w1sc_a, e) if e < EARLY else (w1sc_b, e - EARLY)
+            for e in GROUPS[g]:
+                bank = banks[len(units) % 6]
+                j, at = divmod(e * C, HALF_SLOTS)
                 for s in range(PASSES):
-                    words, scales = gathered[g][s]
-                    at = (first * PASSES + s) * H
+                    w_at = ((e % HALF_E) * PASSES + s) * H
                     nc.tensor.matmul_mx(
-                        out=bank[:], lhsT=words[:, cols].bitcast(FP8X4), lhsT_scale=scales[:, cols],
-                        rhs=w1[g][:, u * PASSES + s, :].bitcast(FP4X4), rhs_scale=plane[:, at:at + H],
+                        out=bank[:], lhsT=slot_words[s][:, e * C:(e + 1) * C].bitcast(FP8X4),
+                        lhsT_scale=(slot_scales, moved_scales)[s][j][:, at:at + C],
+                        rhs=w1_of[e][:, s, :].bitcast(FP4X4), rhs_scale=w1sc[j][:, w_at:w_at + H],
                         start=(s == 0), stop=(s == PASSES - 1))
-                relu_out(g, u, bank)
+                relu_out(g, bank)
 
         def first_layer_shared(j):
             for u in range(2):
-                bank = psum.tile([P, H], F32, name="h_bank", bufs=4)
+                bank = banks[len(units) % 6]
                 t0 = (2 * j + u) * C
                 for s in range(PASSES):
                     nc.tensor.matmul_mx(
-                        out=bank[:], lhsT=xw[s][:, t0:t0 + C].bitcast(FP8X4),
-                        lhsT_scale=xs[:, s * T + t0:s * T + t0 + C],
-                        rhs=w1s[:, s, :].bitcast(FP8X4), rhs_scale=w1ssc[:, s * H:(s + 1) * H],
+                        out=bank[:], lhsT=xw[s][:, t0:t0 + C].bitcast(FP8X4), lhsT_scale=xs[4 * s:P, t0:t0 + C],
+                        rhs=w1s[:, s, :].bitcast(FP8X4), rhs_scale=w1ssc[4 * s:P, :],
                         start=(s == 0), stop=(s == PASSES - 1))
-                relu_out("s%d" % j, u, bank)
+                relu_out("s%d" % j, bank)
 
-        def turn(key):
+        def turn(key, copy):
             tiles = hidden[key]
             n = len(tiles)
-            bank = psum.tile([P, 2, 2, C], F32, name="t_bank", bufs=2)
+            view = banks[6 + len(grouped) % 2][:].rearrange("p (u v j) -> p u v j", u=2, v=2)
             for u, h in enumerate(tiles):
                 pairs = h[:].bitcast(F32)
                 for v in range(2):
-                    nc.tensor.transpose(bank[:, u, v, :], pairs[:, v * P:(v + 1) * P], ident[:])
+                    nc.tensor.transpose(view[:, u, v, :], pairs[:, v * P:(v + 1) * P], ident[:])
             dst = sb("ht%s" % key, [P, n * C * 4], BF16)
-            nc.scalar.copy(
-                dst[:].bitcast(F32).rearrange("p (u j v) -> p u j v", u=n, v=2),
-                bank[:, 0:n].rearrange("p u v j -> p u j v"))
+            copy(dst[:].bitcast(F32).rearrange("p (u j v) -> p u j v", u=n, v=2),
+                 view[:, 0:n].rearrange("p u v j -> p u j v"))
             grouped[key] = dst
 
         def quantise(key, codes, scales):
@@ -176,53 +181,69 @@ def tile_moe_shf_mlp_relu_kernel(
             quantise(g, codes[:], scales[:])
             quantised[g] = (codes, scales)
 
-        def second_layer(g):
-            es = GROUPS[g]
-            codes, scales = quantised[g]
-            bank = psum.tile([P, 2 * C], F32, name="y_bank", bufs=1)
-            for u, e in enumerate(es):
-                cols = slice(u * C, (u + 1) * C)
-                nc.tensor.matmul_mx(
-                    out=bank[:, cols], lhsT=w2[:, e, :].bitcast(FP4X4), lhsT_scale=w2sc[:, e * N:(e + 1) * N],
-                    rhs=codes[:, cols].bitcast(FP8X4), rhs_scale=scales[:, cols], start=True, stop=True)
-            nc.scalar.copy(y_slots[:, es[0] * C:(es[-1] + 1) * C], bank[:, 0:len(es) * C])
-
-        last = len(GROUPS) - 1
-        for i in range(last + 1):
-            gather(i)
-            if i >= 2:
-                quantise_routed(i - 2)
-            first_layer(i)
-            if i >= 2:
-                second_layer(i - 2)
-            turn(i)
-            if i in (3, 4):
-                first_layer_shared(i - 3)
-                turn("s%d" % (i - 3))
-        quantise_routed(last - 1)
-        second_layer(last - 1)
-        quantise_routed(last)
-        second_layer(last)
+        def second_layer(gs, bank, copy):
+            first = GROUPS[gs[0]][0]
+            for g in gs:
+                codes, scales = quantised[g]
+                for u, e in enumerate(GROUPS[g]):
+                    cols = slice(u * C, (u + 1) * C)
+                    nc.tensor.matmul_mx(
+                        out=bank[:, (e - first) * C:(e - first + 1) * C],
+                        lhsT=w2[:, e, :].bitcast(FP4X4), lhsT_scale=w2sc[:, e * N:(e + 1) * N],
+                        rhs=codes[:, cols].bitcast(FP8X4), rhs_scale=scales[:, cols], start=True, stop=True)
+            end = GROUPS[gs[-1]][-1] + 1
+            copy(y_slots[:, first * C:end * C], bank[:, 0:(end - first) * C])
 
         shared_codes = sb("sq", [P, T], U32)
         shared_scales = sb("ss", [P, T], U8)
+
         for j in range(2):
+            first_layer_shared(j)
+        for j in range(2):
+            turn("s%d" % j, nc.scalar.copy)
             cols = slice(j * 2 * C, (j + 1) * 2 * C)
             quantise("s%d" % j, shared_codes[:, cols], shared_scales[:, cols])
-        ys = psum.tile([P, T], F32, name="ys_bank")
+
+        first_layer(0)
+        first_layer(1)
+        first_layer(2)
+        turn(0, nc.scalar.copy)
+        turn(1, nc.vector.tensor_copy)
+        first_layer(3)
+        first_layer(4)
+        quantise_routed(0)
+        quantise_routed(1)
+        turn(2, nc.vector.tensor_copy)
+        turn(3, nc.vector.tensor_copy)
+        first_layer(5)
+        quantise_routed(2)
+        quantise_routed(3)
+        turn(4, nc.vector.tensor_copy)
+        turn(5, nc.vector.tensor_copy)
+        quantise_routed(4)
+        quantise_routed(5)
+        second_layer([0, 1], banks[4], nc.scalar.copy)
+        second_layer([2, 3], banks[5], nc.scalar.copy)
+        second_layer([4], banks[0], nc.scalar.copy)
+        second_layer([5], banks[1], nc.vector.tensor_copy)
+        ys = banks[2]
         nc.tensor.matmul_mx(
             out=ys[:], lhsT=w2s[:].bitcast(FP8X4), lhsT_scale=w2ssc[:],
             rhs=shared_codes[:].bitcast(FP8X4), rhs_scale=shared_scales[:], start=True, stop=True)
 
+        terms = [sb("term%d" % r, [P, T], F32) for r in range(TOP)]
+        sums = [sb("sum%d" % r, [P, T], F32) for r in range(TOP)]
         half = T // 2
+
+        def weigh(r):
+            nc.vector.tensor_tensor(terms[r][:], y_slots[:].indirect(pos_sb[r][:]), gates[r][:], MULT)
+
+        weigh(0)
+        weigh(1)
+        nc.vector.tensor_tensor(sums[0][:], terms[0][:], ys[:], ADD)
+        weigh(2)
+        nc.vector.tensor_tensor(sums[1][:], sums[0][:], terms[1][:], ADD)
         for j in range(2):
             cols = slice(j * half, (j + 1) * half)
-            terms = [sb("term%d_%d" % (j, r), [P, half], F32) for r in range(TOP)]
-            sums = [sb("sum%d_%d" % (j, r), [P, half], F32) for r in range(TOP)]
-            for r in range(TOP):
-                lst = pos_sb[r][:, j * half // 16:(j + 1) * half // 16]
-                nc.vector.tensor_tensor(terms[r][:], y_slots[:].indirect(lst), gates[:, r, cols], MULT)
-            nc.vector.tensor_tensor(sums[0][:], terms[0][:], ys[:, cols], ADD)
-            nc.vector.tensor_tensor(sums[1][:], terms[1][:], terms[2][:], ADD)
-            nc.vector.tensor_tensor(sums[2][:], sums[0][:], sums[1][:], ADD)
-            nc.sync.dma_start(out=out[:, cols], in_=sums[2][:])
+            nc.vector.tensor_tensor(sums[2][:, cols], sums[1][:, cols], terms[2][:, cols], ADD)
+            nc.sync.dma_start(out=out[:, cols], in_=sums[2][:, cols])

@@ -23,10 +23,11 @@ MULT = mybir.AluOpType.mult
 ADD = mybir.AluOpType.add
 
 GROUPS = [[0, 1], [2, 3], [4, 5], [6, 7], [8, 9], [10, 11]]
-WORD_LOADS = [(0, 2), (2, 4), (4, 6), (6, 8), (8, 10), (10, 11), (11, 12)]
-HALF_E = E // 2
-HALF_SLOTS = SLOTS // 2
+WORD_LOADS = [(0, 3), (3, 6), (6, 9), (9, 11), (11, 12)]
+SCALE_LOADS = [(0, 3), (3, 12)]
+SCALE_MOVES = [(0, 384), (384, 1152)]
 PIECE = 384
+WORD_GATHERS = [(0, 256), (256, 256), (512, 256), (768, 384), (1152, 384)]
 MOVED = 112
 
 
@@ -57,69 +58,84 @@ def tile_moe_shf_mlp_relu_kernel(
 
         offs_sb = keep.tile([P, SLOTS // 16], U16, name="offs_sb")
         pos_sb = [keep.tile([P, T // 16], U16, name="pos%d_sb" % r) for r in range(TOP)]
-        xw = [sb("xw%d" % s, [P, T], I32) for s in range(PASSES)]
+        xw = sb("xw", [P, PASSES, T], I32)
         xs = sb("xs", [P, T], U8)
         w1 = [sb("w1_%d" % lo, [P, (hi - lo) * PASSES, 2 * H], U8) for lo, hi in WORD_LOADS]
-        w1sc = [sb("w1sc_%d" % j, [P, HALF_E * PASSES * H], U8) for j in range(2)]
+        w1sc = [sb("w1sc_%d" % lo, [P, (hi - lo) * PASSES * H], U8) for lo, hi in SCALE_LOADS]
         w2 = sb("w2", [P, E, 2 * N], U8)
         w2sc = sb("w2sc", [P, E * N], U8)
         w1s = sb("w1s", [P, PASSES, H], I32)
         w1ssc = sb("w1ssc", [P, H], U8)
         w2s = sb("w2s", [P, N], I32)
         w2ssc = sb("w2ssc", [P, N], U8)
-        gates = [sb("gate%d" % r, [P, T], F32) for r in range(TOP)]
+        gate_first = sb("gate_first", [P, T], F32)
+        gate_rest = sb("gate_rest", [P, TOP - 1, T], F32)
+        gates = [gate_first[:], gate_rest[:, 0, :], gate_rest[:, 1, :]]
         ident = sb("ident", [P, P], F32)
-        warm = sb("warm", [P, 1], F32)
+        warm = sb("warm", [P, 2], F32)
         y_slots = sb("y_slots", [P, SLOTS], F32)
         slot_words = [sb("slot_words%d" % s, [P, SLOTS], U32) for s in range(PASSES)]
-        slot_scales = [sb("slot_scales%d" % j, [P, HALF_SLOTS], U8) for j in range(2)]
-        moved_scales = [sb("moved_scales%d" % j, [P, HALF_SLOTS], U8) for j in range(2)]
+        slot_scales = [sb("slot_scales%d" % at, [P, count], U8) for at, count in SCALE_MOVES]
+        moved_scales = [sb("moved_scales%d" % at, [P, count], U8) for at, count in SCALE_MOVES]
         banks = [psum.tile([P, H], F32, name="bank%d" % b) for b in range(8)]
 
-        for plane in (xs, w1ssc, w1sc[0]):
-            nc.vector.memset(plane[:].bitcast(I32), 0)
+        nc.vector.memset(warm[:, 0:1], 0.0)
+        nc.scalar.activation(warm[:, 1:2], warm[:, 0:1], RELU)
         make_identity(nc, ident[:])
-        for plane in (w1sc[1], moved_scales[0], moved_scales[1], w2sc, w2ssc):
-            nc.gpsimd.memset(plane[:].bitcast(I32), 0)
-        nc.scalar.activation(warm[:], ident[:, 0:1], RELU)
+        for plane in (xs, w1sc[0], moved_scales[0], w1sc[1], w2sc, w1ssc, moved_scales[1], w2ssc):
+            nc.vector.memset(plane[:].bitcast(I32), 0)
 
-        nc.sync.dma_start(offs_sb[:], offs)
-        load_packed_scale_rows(nc.sync, xs[:], x_scales)
-        load_packed_scale_rows(nc.sync, w1ssc[:], w1s_scales)
-        for s in range(PASSES):
-            nc.sync.dma_start(out=xw[s][:], in_=x_words[s].rearrange("p t d -> p (t d)").bitcast(I32))
-        nc.sync.dma_start(out=w1s[:], in_=w1s_words.rearrange("s p l d -> p s (l d)").bitcast(I32))
-        for j in range(2):
-            rows = w1_scales[j * HALF_E:(j + 1) * HALF_E].rearrange("e s b i -> (e s) b i")
-            load_scale_rows(nc.sync, w1sc[j][:], rows)
         w1_of = {}
-        for tile, (lo, hi) in zip(w1, WORD_LOADS):
+
+        def load_w1_words(j):
+            lo, hi = WORD_LOADS[j]
             src = w1_words[lo:hi].bitcast(I32).rearrange("e s p c -> p (e s) c")
-            nc.sync.dma_start(out=tile[:].bitcast(I32), in_=src)
+            nc.sync.dma_start(out=w1[j][:].bitcast(I32), in_=src)
             for e in range(lo, hi):
-                w1_of[e] = tile[:, (e - lo) * PASSES:(e - lo + 1) * PASSES, :]
-        load_scale_rows(nc.sync, w2sc[:], w2_scales.rearrange("e s b n -> (e s) b n"))
-        nc.sync.dma_start(out=w2[:].bitcast(I32), in_=w2_words.bitcast(I32).rearrange("e s p c -> p (e s) c"))
-        for r, pos in enumerate((pos1, pos2, pos3)):
-            nc.sync.dma_start(pos_sb[r][:], pos)
-        for r in range(TOP):
-            nc.sync.dma_start(out=gates[r][:], in_=gate[r])
-        load_scale_rows(nc.sync, w2ssc[:], w2s_scales)
-        nc.sync.dma_start(out=w2s[:], in_=w2s_words[0].rearrange("p n d -> p (n d)").bitcast(I32))
+                w1_of[e] = w1[j][:, (e - lo) * PASSES:(e - lo + 1) * PASSES, :]
+
+        def load_w1_scales(queue, j):
+            lo, hi = SCALE_LOADS[j]
+            load_scale_rows(queue, w1sc[j][:], w1_scales[lo:hi].rearrange("e s b i -> (e s) b i"))
 
         def slot_list(first, count):
             return offs_sb[:, first // 16:(first + count) // 16]
 
-        for j in range(2):
-            for at in range(0, HALF_SLOTS, PIECE):
-                nc.vector.tensor_copy(slot_scales[j][:, at:at + PIECE],
-                                      xs[:].indirect(slot_list(j * HALF_SLOTS + at, PIECE)))
-            nc.scalar.dma_start(out=moved_scales[j][:].bitcast(I32)[0:MOVED, :],
-                                in_=slot_scales[j][:].bitcast(I32)[4:4 + MOVED, :])
-        for at in range(0, SLOTS, PIECE):
+        def gather_scales(j):
+            first, count = SCALE_MOVES[j]
+            for at in range(0, count, PIECE):
+                nc.vector.tensor_copy(slot_scales[j][:, at:at + PIECE], xs[:].indirect(slot_list(first + at, PIECE)))
+            nc.sync.dma_start(out=moved_scales[j][:].bitcast(I32)[0:MOVED, :],
+                              in_=slot_scales[j][:].bitcast(I32)[4:4 + MOVED, :])
+
+        nc.sync.dma_start(offs_sb[:], offs)
+        load_packed_scale_rows(nc.sync, xs[:], x_scales)
+        nc.sync.dma_start(out=xw[:], in_=x_words.rearrange("s p t d -> p s (t d)").bitcast(I32))
+        load_w1_scales(nc.sync, 0)
+        load_w1_words(0)
+        gather_scales(0)
+        load_w1_words(1)
+        gather_scales(1)
+        load_w1_words(2)
+        load_w1_words(3)
+        load_w1_words(4)
+        nc.sync.dma_start(out=w2[:].bitcast(I32), in_=w2_words.bitcast(I32).rearrange("e s p c -> p (e s) c"))
+        nc.sync.dma_start(out=w1s[:], in_=w1s_words.rearrange("s p l d -> p s (l d)").bitcast(I32))
+        for r, pos in enumerate((pos1, pos2, pos3)):
+            nc.sync.dma_start(pos_sb[r][:], pos)
+        nc.sync.dma_start(out=gate_first[:], in_=gate[0])
+        nc.sync.dma_start(out=gate_rest[:], in_=gate[1:TOP].rearrange("r p t -> p r t"))
+        nc.sync.dma_start(out=w2s[:], in_=w2s_words[0].rearrange("p n d -> p (n d)").bitcast(I32))
+
+        load_w1_scales(nc.gpsimd, 1)
+        load_scale_rows(nc.gpsimd, w2sc[:], w2_scales.rearrange("e s b n -> (e s) b n"))
+        load_packed_scale_rows(nc.gpsimd, w1ssc[:], w1s_scales)
+        load_scale_rows(nc.gpsimd, w2ssc[:], w2s_scales)
+
+        for at, count in WORD_GATHERS:
             for s in range(PASSES):
-                nc.vector.tensor_copy(slot_words[s][:, at:at + PIECE],
-                                      xw[s][:].bitcast(U32).indirect(slot_list(at, PIECE)))
+                nc.vector.tensor_copy(slot_words[s][:, at:at + count],
+                                      xw[:, s, :].bitcast(U32).indirect(slot_list(at, count)))
 
         hidden = {}
         grouped = {}
@@ -137,9 +153,10 @@ def tile_moe_shf_mlp_relu_kernel(
         def first_layer(g):
             for e in GROUPS[g]:
                 bank = banks[len(units) % 6]
-                j, at = divmod(e * C, HALF_SLOTS)
+                j = int(e * C >= SCALE_MOVES[1][0])
+                at = e * C - SCALE_MOVES[j][0]
                 for s in range(PASSES):
-                    w_at = ((e % HALF_E) * PASSES + s) * H
+                    w_at = ((e - SCALE_LOADS[j][0]) * PASSES + s) * H
                     nc.tensor.matmul_mx(
                         out=bank[:], lhsT=slot_words[s][:, e * C:(e + 1) * C].bitcast(FP8X4),
                         lhsT_scale=(slot_scales, moved_scales)[s][j][:, at:at + C],
@@ -149,19 +166,19 @@ def tile_moe_shf_mlp_relu_kernel(
 
         def first_layer_shared(j):
             for u in range(2):
-                bank = banks[len(units) % 6]
+                bank = banks[4 + 2 * j + u]
                 t0 = (2 * j + u) * C
                 for s in range(PASSES):
                     nc.tensor.matmul_mx(
-                        out=bank[:], lhsT=xw[s][:, t0:t0 + C].bitcast(FP8X4), lhsT_scale=xs[4 * s:P, t0:t0 + C],
+                        out=bank[:], lhsT=xw[:, s, t0:t0 + C].bitcast(FP8X4), lhsT_scale=xs[4 * s:P, t0:t0 + C],
                         rhs=w1s[:, s, :].bitcast(FP8X4), rhs_scale=w1ssc[4 * s:P, :],
                         start=(s == 0), stop=(s == PASSES - 1))
                 relu_out("s%d" % j, bank)
 
-        def turn(key, copy):
+        def turn(key, bank, copy):
             tiles = hidden[key]
             n = len(tiles)
-            view = banks[6 + len(grouped) % 2][:].rearrange("p (u v j) -> p u v j", u=2, v=2)
+            view = bank[:].rearrange("p (u v j) -> p u v j", u=2, v=2)
             for u, h in enumerate(tiles):
                 pairs = h[:].bitcast(F32)
                 for v in range(2):
@@ -194,56 +211,53 @@ def tile_moe_shf_mlp_relu_kernel(
             end = GROUPS[gs[-1]][-1] + 1
             copy(y_slots[:, first * C:end * C], bank[:, 0:(end - first) * C])
 
-        shared_codes = sb("sq", [P, T], U32)
-        shared_scales = sb("ss", [P, T], U8)
-
-        for j in range(2):
-            first_layer_shared(j)
-        for j in range(2):
-            turn("s%d" % j, nc.scalar.copy)
-            cols = slice(j * 2 * C, (j + 1) * 2 * C)
-            quantise("s%d" % j, shared_codes[:, cols], shared_scales[:, cols])
+        shared_codes = [sb("sq%d" % j, [P, T // 2], U32) for j in range(2)]
+        shared_scales = [sb("ss%d" % j, [P, T // 2], U8) for j in range(2)]
 
         first_layer(0)
         first_layer(1)
         first_layer(2)
-        turn(0, nc.scalar.copy)
-        turn(1, nc.vector.tensor_copy)
+        turn(0, banks[6], nc.scalar.copy)
+        turn(1, banks[7], nc.scalar.copy)
         first_layer(3)
+        turn(2, banks[6], nc.vector.tensor_copy)
         first_layer(4)
         quantise_routed(0)
         quantise_routed(1)
-        turn(2, nc.vector.tensor_copy)
-        turn(3, nc.vector.tensor_copy)
+        turn(3, banks[7], nc.vector.tensor_copy)
         first_layer(5)
         quantise_routed(2)
         quantise_routed(3)
-        turn(4, nc.vector.tensor_copy)
-        turn(5, nc.vector.tensor_copy)
+        turn(4, banks[6], nc.vector.tensor_copy)
+        turn(5, banks[7], nc.vector.tensor_copy)
         quantise_routed(4)
         quantise_routed(5)
         second_layer([0, 1], banks[4], nc.scalar.copy)
         second_layer([2, 3], banks[5], nc.scalar.copy)
-        second_layer([4], banks[0], nc.scalar.copy)
-        second_layer([5], banks[1], nc.vector.tensor_copy)
-        ys = banks[2]
-        nc.tensor.matmul_mx(
-            out=ys[:], lhsT=w2s[:].bitcast(FP8X4), lhsT_scale=w2ssc[:],
-            rhs=shared_codes[:].bitcast(FP8X4), rhs_scale=shared_scales[:], start=True, stop=True)
+        second_layer([4], banks[6], nc.scalar.copy)
+        second_layer([5], banks[7], nc.vector.tensor_copy)
+        for j in range(2):
+            first_layer_shared(j)
+        for j in range(2):
+            turn("s%d" % j, banks[j], nc.scalar.copy)
 
         terms = [sb("term%d" % r, [P, T], F32) for r in range(TOP)]
-        sums = [sb("sum%d" % r, [P, T], F32) for r in range(TOP)]
+        sums = [sb("sum_two", [P, T], F32), grouped["s1"][:].bitcast(F32), sb("result", [P, T], F32)]
         half = T // 2
 
-        def weigh(r):
-            nc.vector.tensor_tensor(terms[r][:], y_slots[:].indirect(pos_sb[r][:]), gates[r][:], MULT)
+        def shared_second_layer(j):
+            quantise("s%d" % j, shared_codes[j][:], shared_scales[j][:])
+            nc.tensor.matmul_mx(
+                out=banks[2 + j][:, 0:half], lhsT=w2s[:].bitcast(FP8X4), lhsT_scale=w2ssc[:],
+                rhs=shared_codes[j][:].bitcast(FP8X4), rhs_scale=shared_scales[j][:], start=True, stop=True)
 
-        weigh(0)
-        weigh(1)
-        nc.vector.tensor_tensor(sums[0][:], terms[0][:], ys[:], ADD)
-        weigh(2)
-        nc.vector.tensor_tensor(sums[1][:], sums[0][:], terms[1][:], ADD)
+        for r in range(TOP):
+            nc.vector.tensor_tensor(terms[r][:], y_slots[:].indirect(pos_sb[r][:]), gates[r], MULT)
+        nc.vector.tensor_tensor(sums[0][:], terms[0][:], terms[1][:], ADD)
+        shared_second_layer(0)
+        shared_second_layer(1)
+        nc.vector.tensor_tensor(sums[1], sums[0][:], terms[2][:], ADD)
         for j in range(2):
             cols = slice(j * half, (j + 1) * half)
-            nc.vector.tensor_tensor(sums[2][:, cols], sums[1][:, cols], terms[2][:, cols], ADD)
+            nc.vector.tensor_tensor(sums[2][:, cols], sums[1][:, cols], banks[2 + j][:, 0:half], ADD)
             nc.sync.dma_start(out=out[:, cols], in_=sums[2][:, cols])

@@ -22,13 +22,8 @@ RELU = mybir.ActivationFunctionType.Relu
 MULT = mybir.AluOpType.mult
 ADD = mybir.AluOpType.add
 
-GROUPS = [[0, 1], [2, 3], [4, 5], [6, 7], [8, 9], [10, 11]]
-WORD_LOADS = [(0, 3), (3, 6), (6, 9), (9, 11), (11, 12)]
-SCALE_LOADS = [(0, 3), (3, 12)]
-SCALE_MOVES = [(0, 384), (384, 1152)]
-PIECE = 384
-WORD_GATHERS = [(0, 256), (256, 256), (512, 256), (768, 384), (1152, 384)]
-MOVED = 112
+GROUPS = [(0, 2), (2, 4), (4, 6), (6, 8), (8, 10), (10, 11), (11, 12)]
+RUN = 4
 
 
 def load_scale_rows(queue, plane, rows):
@@ -37,11 +32,6 @@ def load_scale_rows(queue, plane, rows):
     dst = plane.bitcast(I32).rearrange("p (b w) -> p b w", b=blocks)
     for r in range(4):
         queue.dma_start(out=dst[r:P:32], in_=src[r])
-
-
-def load_packed_scale_rows(queue, plane, rows):
-    for q in range(4):
-        queue.dma_start(out=plane.bitcast(I32)[32 * q:32 * q + 8, :], in_=rows.bitcast(I32)[:, 4 * q:4 * q + 4, :])
 
 
 def tile_moe_shf_mlp_relu_kernel(
@@ -58,129 +48,118 @@ def tile_moe_shf_mlp_relu_kernel(
 
         offs_sb = keep.tile([P, SLOTS // 16], U16, name="offs_sb")
         pos_sb = [keep.tile([P, T // 16], U16, name="pos%d_sb" % r) for r in range(TOP)]
-        xw = sb("xw", [P, PASSES, T], I32)
-        xs = sb("xs", [P, T], U8)
-        w1 = [sb("w1_%d" % lo, [P, (hi - lo) * PASSES, 2 * H], U8) for lo, hi in WORD_LOADS]
-        w1sc = [sb("w1sc_%d" % lo, [P, (hi - lo) * PASSES * H], U8) for lo, hi in SCALE_LOADS]
+        xw = [sb("xw%d" % s, [P, T], I32) for s in range(PASSES)]
+        xs = sb("xs", [P, PASSES * T], U8)
+        w1 = [sb("w1_%d" % lo, [P, (hi - lo) * PASSES, 2 * H], U8) for lo, hi in GROUPS]
+        w1sc = [sb("w1sc_%d" % j, [P, RUN * PASSES * H], U8) for j in range(E // RUN)]
         w2 = sb("w2", [P, E, 2 * N], U8)
         w2sc = sb("w2sc", [P, E * N], U8)
         w1s = sb("w1s", [P, PASSES, H], I32)
-        w1ssc = sb("w1ssc", [P, H], U8)
+        w1ssc = sb("w1ssc", [P, PASSES * H], U8)
         w2s = sb("w2s", [P, N], I32)
         w2ssc = sb("w2ssc", [P, N], U8)
         gate_first = sb("gate_first", [P, T], F32)
         gate_rest = sb("gate_rest", [P, TOP - 1, T], F32)
         gates = [gate_first[:], gate_rest[:, 0, :], gate_rest[:, 1, :]]
+        ident_raw = sb("ident_raw", [P, P], F32)
         ident = sb("ident", [P, P], F32)
-        warm = sb("warm", [P, 2], F32)
         y_slots = sb("y_slots", [P, SLOTS], F32)
         slot_words = [sb("slot_words%d" % s, [P, SLOTS], U32) for s in range(PASSES)]
-        slot_scales = [sb("slot_scales%d" % at, [P, count], U8) for at, count in SCALE_MOVES]
-        moved_scales = [sb("moved_scales%d" % at, [P, count], U8) for at, count in SCALE_MOVES]
+        slot_scales = [sb("slot_scales%d" % s, [P, SLOTS], U8) for s in range(PASSES)]
         banks = [psum.tile([P, H], F32, name="bank%d" % b) for b in range(8)]
 
-        nc.vector.memset(warm[:, 0:1], 0.0)
-        nc.scalar.activation(warm[:, 1:2], warm[:, 0:1], RELU)
-        make_identity(nc, ident[:])
-        for plane in (xs, w1sc[0], moved_scales[0], w1sc[1], w2sc, w1ssc, moved_scales[1], w2ssc):
+        make_identity(nc, ident_raw[:])
+        nc.scalar.activation(ident[:], ident_raw[:], RELU)
+        for plane in [xs] + w1sc + [w2sc, w1ssc, w2ssc]:
             nc.vector.memset(plane[:].bitcast(I32), 0)
 
-        w1_of = {}
+        def load_x_words(s):
+            nc.sync.dma_start(out=xw[s][:], in_=x_words[s].rearrange("p t d -> p (t d)").bitcast(I32))
 
-        def load_w1_words(j):
-            lo, hi = WORD_LOADS[j]
+        def load_w1_words(g):
+            lo, hi = GROUPS[g]
             src = w1_words[lo:hi].bitcast(I32).rearrange("e s p c -> p (e s) c")
-            nc.sync.dma_start(out=w1[j][:].bitcast(I32), in_=src)
-            for e in range(lo, hi):
-                w1_of[e] = w1[j][:, (e - lo) * PASSES:(e - lo + 1) * PASSES, :]
+            nc.sync.dma_start(out=w1[g][:].bitcast(I32), in_=src)
 
-        def load_w1_scales(queue, j):
-            lo, hi = SCALE_LOADS[j]
-            load_scale_rows(queue, w1sc[j][:], w1_scales[lo:hi].rearrange("e s b i -> (e s) b i"))
+        def load_w1_scales(j):
+            load_scale_rows(nc.sync, w1sc[j][:], w1_scales[j * RUN:(j + 1) * RUN].rearrange("e s b i -> (e s) b i"))
 
-        def slot_list(first, count):
-            return offs_sb[:, first // 16:(first + count) // 16]
-
-        def gather_scales(j):
-            first, count = SCALE_MOVES[j]
-            for at in range(0, count, PIECE):
-                nc.vector.tensor_copy(slot_scales[j][:, at:at + PIECE], xs[:].indirect(slot_list(first + at, PIECE)))
-            nc.sync.dma_start(out=moved_scales[j][:].bitcast(I32)[0:MOVED, :],
-                              in_=slot_scales[j][:].bitcast(I32)[4:4 + MOVED, :])
-
+        load_x_words(0)
+        load_scale_rows(nc.sync, xs[:], x_scales)
         nc.sync.dma_start(offs_sb[:], offs)
-        load_packed_scale_rows(nc.sync, xs[:], x_scales)
-        nc.sync.dma_start(out=xw[:], in_=x_words.rearrange("s p t d -> p s (t d)").bitcast(I32))
-        load_w1_scales(nc.sync, 0)
+        load_x_words(1)
         load_w1_words(0)
-        gather_scales(0)
+        load_w1_scales(0)
         load_w1_words(1)
-        gather_scales(1)
         load_w1_words(2)
+        load_w1_scales(1)
         load_w1_words(3)
-        load_w1_words(4)
-        nc.sync.dma_start(out=w2[:].bitcast(I32), in_=w2_words.bitcast(I32).rearrange("e s p c -> p (e s) c"))
-        nc.sync.dma_start(out=w1s[:], in_=w1s_words.rearrange("s p l d -> p s (l d)").bitcast(I32))
         for r, pos in enumerate((pos1, pos2, pos3)):
             nc.sync.dma_start(pos_sb[r][:], pos)
+        load_w1_words(4)
+        load_w1_scales(2)
+        load_scale_rows(nc.sync, w2sc[:], w2_scales.rearrange("e s b n -> (e s) b n"))
+        load_w1_words(5)
+        load_w1_words(6)
+        nc.sync.dma_start(out=w2[:].bitcast(I32), in_=w2_words.bitcast(I32).rearrange("e s p c -> p (e s) c"))
+        nc.sync.dma_start(out=w1s[:], in_=w1s_words.rearrange("s p l d -> p s (l d)").bitcast(I32))
+        load_scale_rows(nc.sync, w1ssc[:], w1s_scales)
         nc.sync.dma_start(out=gate_first[:], in_=gate[0])
         nc.sync.dma_start(out=gate_rest[:], in_=gate[1:TOP].rearrange("r p t -> p r t"))
         nc.sync.dma_start(out=w2s[:], in_=w2s_words[0].rearrange("p n d -> p (n d)").bitcast(I32))
+        load_scale_rows(nc.sync, w2ssc[:], w2s_scales)
 
-        load_w1_scales(nc.gpsimd, 1)
-        load_scale_rows(nc.gpsimd, w2sc[:], w2_scales.rearrange("e s b n -> (e s) b n"))
-        load_packed_scale_rows(nc.gpsimd, w1ssc[:], w1s_scales)
-        load_scale_rows(nc.gpsimd, w2ssc[:], w2s_scales)
-
-        for at, count in WORD_GATHERS:
+        for lo, hi in GROUPS:
+            cols = slice(lo * C, hi * C)
+            entries = offs_sb[:, lo * C // 16:hi * C // 16]
+            nc.vector.tensor_copy(slot_words[0][:, cols], xw[0][:].bitcast(U32).indirect(entries))
             for s in range(PASSES):
-                nc.vector.tensor_copy(slot_words[s][:, at:at + count],
-                                      xw[:, s, :].bitcast(U32).indirect(slot_list(at, count)))
+                nc.vector.tensor_copy(slot_scales[s][:, cols], xs[:, s * T:(s + 1) * T].indirect(entries))
+            nc.vector.tensor_copy(slot_words[1][:, cols], xw[1][:].bitcast(U32).indirect(entries))
 
         hidden = {}
         grouped = {}
         quantised = {}
-        units = []
 
-        def relu_out(key, bank):
-            h = sb("h%d" % len(units), [P, H], BF16)
+        def relu_out(h, bank):
             nc.scalar.activation(
-                h[:].rearrange("p (v m d) -> p v m d", v=2, d=2),
+                h.rearrange("p (v m d) -> p v m d", v=2, d=2),
                 bank[:].rearrange("p (m v d) -> p v m d", v=2, d=2), RELU)
-            hidden.setdefault(key, []).append(h)
-            units.append(key)
 
         def first_layer(g):
-            for e in GROUPS[g]:
-                bank = banks[len(units) % 6]
-                j = int(e * C >= SCALE_MOVES[1][0])
-                at = e * C - SCALE_MOVES[j][0]
+            lo, hi = GROUPS[g]
+            hidden[g] = sb("h%d" % g, [P, hi - lo, H], BF16)
+            for e in range(lo, hi):
+                bank = banks[e % 4]
                 for s in range(PASSES):
-                    w_at = ((e - SCALE_LOADS[j][0]) * PASSES + s) * H
+                    w_at = ((e % RUN) * PASSES + s) * H
                     nc.tensor.matmul_mx(
                         out=bank[:], lhsT=slot_words[s][:, e * C:(e + 1) * C].bitcast(FP8X4),
-                        lhsT_scale=(slot_scales, moved_scales)[s][j][:, at:at + C],
-                        rhs=w1_of[e][:, s, :].bitcast(FP4X4), rhs_scale=w1sc[j][:, w_at:w_at + H],
+                        lhsT_scale=slot_scales[s][:, e * C:(e + 1) * C],
+                        rhs=w1[g][:, (e - lo) * PASSES + s, :].bitcast(FP4X4),
+                        rhs_scale=w1sc[e // RUN][:, w_at:w_at + H],
                         start=(s == 0), stop=(s == PASSES - 1))
-                relu_out(g, bank)
+                relu_out(hidden[g][:, e - lo, :], bank)
 
         def first_layer_shared(j):
+            key = "s%d" % j
+            hidden[key] = sb("h" + key, [P, 2, H], BF16)
             for u in range(2):
-                bank = banks[4 + 2 * j + u]
+                bank = banks[2 * j + u]
                 t0 = (2 * j + u) * C
                 for s in range(PASSES):
                     nc.tensor.matmul_mx(
-                        out=bank[:], lhsT=xw[:, s, t0:t0 + C].bitcast(FP8X4), lhsT_scale=xs[4 * s:P, t0:t0 + C],
-                        rhs=w1s[:, s, :].bitcast(FP8X4), rhs_scale=w1ssc[4 * s:P, :],
+                        out=bank[:], lhsT=xw[s][:, t0:t0 + C].bitcast(FP8X4),
+                        lhsT_scale=xs[:, s * T + t0:s * T + t0 + C],
+                        rhs=w1s[:, s, :].bitcast(FP8X4), rhs_scale=w1ssc[:, s * H:(s + 1) * H],
                         start=(s == 0), stop=(s == PASSES - 1))
-                relu_out("s%d" % j, bank)
+                relu_out(hidden[key][:, u, :], bank)
 
         def turn(key, bank, copy):
-            tiles = hidden[key]
-            n = len(tiles)
+            n = hidden[key].shape[1]
             view = bank[:].rearrange("p (u v j) -> p u v j", u=2, v=2)
-            for u, h in enumerate(tiles):
-                pairs = h[:].bitcast(F32)
+            for u in range(n):
+                pairs = hidden[key][:, u, :].bitcast(F32)
                 for v in range(2):
                     nc.tensor.transpose(view[:, u, v, :], pairs[:, v * P:(v + 1) * P], ident[:])
             dst = sb("ht%s" % key, [P, n * C * 4], BF16)
@@ -188,68 +167,53 @@ def tile_moe_shf_mlp_relu_kernel(
                  view[:, 0:n].rearrange("p u v j -> p u j v"))
             grouped[key] = dst
 
-        def quantise(key, codes, scales):
-            nc.vector.quantize_mx(out=codes.bitcast(FP8X4), scales=scales, in_=grouped[key][:])
-
-        def quantise_routed(g):
-            n = len(GROUPS[g]) * C
-            codes = sb("hq%d" % g, [P, n], U32)
-            scales = sb("hs%d" % g, [P, n], U8)
-            quantise(g, codes[:], scales[:])
-            quantised[g] = (codes, scales)
+        def quantise(key):
+            n = hidden[key].shape[1] * C
+            codes = sb("hq%s" % key, [P, n], U32)
+            scales = sb("hsc%s" % key, [P, n], U8)
+            nc.vector.quantize_mx(out=codes[:].bitcast(FP8X4), scales=scales[:], in_=grouped[key][:])
+            quantised[key] = (codes, scales)
 
         def second_layer(gs, bank, copy):
             first = GROUPS[gs[0]][0]
             for g in gs:
                 codes, scales = quantised[g]
-                for u, e in enumerate(GROUPS[g]):
-                    cols = slice(u * C, (u + 1) * C)
+                lo, hi = GROUPS[g]
+                for e in range(lo, hi):
+                    cols = slice((e - lo) * C, (e - lo + 1) * C)
                     nc.tensor.matmul_mx(
                         out=bank[:, (e - first) * C:(e - first + 1) * C],
                         lhsT=w2[:, e, :].bitcast(FP4X4), lhsT_scale=w2sc[:, e * N:(e + 1) * N],
                         rhs=codes[:, cols].bitcast(FP8X4), rhs_scale=scales[:, cols], start=True, stop=True)
-            end = GROUPS[gs[-1]][-1] + 1
+            end = GROUPS[gs[-1]][1]
             copy(y_slots[:, first * C:end * C], bank[:, 0:(end - first) * C])
 
-        shared_codes = [sb("sq%d" % j, [P, T // 2], U32) for j in range(2)]
-        shared_scales = [sb("ss%d" % j, [P, T // 2], U8) for j in range(2)]
-
         first_layer(0)
-        first_layer(1)
-        first_layer(2)
-        turn(0, banks[6], nc.scalar.copy)
-        turn(1, banks[7], nc.scalar.copy)
-        first_layer(3)
-        turn(2, banks[6], nc.vector.tensor_copy)
-        first_layer(4)
-        quantise_routed(0)
-        quantise_routed(1)
-        turn(3, banks[7], nc.vector.tensor_copy)
-        first_layer(5)
-        quantise_routed(2)
-        quantise_routed(3)
-        turn(4, banks[6], nc.vector.tensor_copy)
-        turn(5, banks[7], nc.vector.tensor_copy)
-        quantise_routed(4)
-        quantise_routed(5)
-        second_layer([0, 1], banks[4], nc.scalar.copy)
-        second_layer([2, 3], banks[5], nc.scalar.copy)
-        second_layer([4], banks[6], nc.scalar.copy)
-        second_layer([5], banks[7], nc.vector.tensor_copy)
+        for g in range(1, len(GROUPS)):
+            first_layer(g)
+            turn(g - 1, banks[4 + g % 2], nc.scalar.copy)
+        turn(len(GROUPS) - 1, banks[4 + len(GROUPS) % 2], nc.scalar.copy)
+        for g in range(len(GROUPS)):
+            quantise(g)
+        second_layer([0, 1], banks[6], nc.scalar.copy)
+        second_layer([2, 3], banks[7], nc.vector.tensor_copy)
+        second_layer([4, 5], banks[0], nc.scalar.copy)
+        second_layer([6], banks[1], nc.vector.tensor_copy)
         for j in range(2):
             first_layer_shared(j)
         for j in range(2):
-            turn("s%d" % j, banks[j], nc.scalar.copy)
+            turn("s%d" % j, banks[4 + j], nc.scalar.copy)
 
         terms = [sb("term%d" % r, [P, T], F32) for r in range(TOP)]
         sums = [sb("sum_two", [P, T], F32), grouped["s1"][:].bitcast(F32), sb("result", [P, T], F32)]
         half = T // 2
 
         def shared_second_layer(j):
-            quantise("s%d" % j, shared_codes[j][:], shared_scales[j][:])
+            quantise("s%d" % j)
+            codes, scales = quantised["s%d" % j]
             nc.tensor.matmul_mx(
-                out=banks[2 + j][:, 0:half], lhsT=w2s[:].bitcast(FP8X4), lhsT_scale=w2ssc[:],
-                rhs=shared_codes[j][:].bitcast(FP8X4), rhs_scale=shared_scales[j][:], start=True, stop=True)
+                out=banks[6 + j][:, 0:half], lhsT=w2s[:].bitcast(FP8X4), lhsT_scale=w2ssc[:],
+                rhs=codes[:].bitcast(FP8X4), rhs_scale=scales[:], start=True, stop=True)
 
         for r in range(TOP):
             nc.vector.tensor_tensor(terms[r][:], y_slots[:].indirect(pos_sb[r][:]), gates[r], MULT)
@@ -259,5 +223,5 @@ def tile_moe_shf_mlp_relu_kernel(
         nc.vector.tensor_tensor(sums[1], sums[0][:], terms[2][:], ADD)
         for j in range(2):
             cols = slice(j * half, (j + 1) * half)
-            nc.vector.tensor_tensor(sums[2][:, cols], sums[1][:, cols], banks[2 + j][:, 0:half], ADD)
+            nc.vector.tensor_tensor(sums[2][:, cols], sums[1][:, cols], banks[6 + j][:, 0:half], ADD)
             nc.sync.dma_start(out=out[:, cols], in_=sums[2][:, cols])

@@ -22,7 +22,9 @@ RELU = mybir.ActivationFunctionType.Relu
 MULT = mybir.AluOpType.mult
 ADD = mybir.AluOpType.add
 
-GROUPS = [(0, 2), (2, 4), (4, 6), (6, 8), (8, 10), (10, 11), (11, 12)]
+PAIRS = [(e, e + 2) for e in range(0, E, 2)]
+GATHERS = PAIRS[:-1] + [(E - 2, E - 1), (E - 1, E)]
+TURNS = [(0, 1)] + [(e, e + 2) for e in range(1, E - 1, 2)] + [(E - 1, E)]
 RUN = 4
 
 
@@ -50,7 +52,7 @@ def tile_moe_shf_mlp_relu_kernel(
         pos_sb = [keep.tile([P, T // 16], U16, name="pos%d_sb" % r) for r in range(TOP)]
         xw = [sb("xw%d" % s, [P, T], I32) for s in range(PASSES)]
         xs = sb("xs", [P, PASSES * T], U8)
-        w1 = [sb("w1_%d" % lo, [P, (hi - lo) * PASSES, 2 * H], U8) for lo, hi in GROUPS]
+        w1 = [sb("w1_%d" % lo, [P, (hi - lo) * PASSES, 2 * H], U8) for lo, hi in PAIRS]
         w1sc = [sb("w1sc_%d" % j, [P, RUN * PASSES * H], U8) for j in range(E // RUN)]
         w2 = sb("w2", [P, E, 2 * N], U8)
         w2sc = sb("w2sc", [P, E * N], U8)
@@ -58,9 +60,8 @@ def tile_moe_shf_mlp_relu_kernel(
         w1ssc = sb("w1ssc", [P, PASSES * H], U8)
         w2s = sb("w2s", [P, N], I32)
         w2ssc = sb("w2ssc", [P, N], U8)
-        gate_first = sb("gate_first", [P, T], F32)
-        gate_rest = sb("gate_rest", [P, TOP - 1, T], F32)
-        gates = [gate_first[:], gate_rest[:, 0, :], gate_rest[:, 1, :]]
+        gate_cols = sb("gate_cols", [P, TOP, T // P], F32)
+        gates = [sb("gate%d" % r, [P, T], F32) for r in range(TOP)]
         ident_raw = sb("ident_raw", [P, P], F32)
         ident = sb("ident", [P, P], F32)
         y_slots = sb("y_slots", [P, SLOTS], F32)
@@ -69,7 +70,6 @@ def tile_moe_shf_mlp_relu_kernel(
         banks = [psum.tile([P, H], F32, name="bank%d" % b) for b in range(8)]
 
         make_identity(nc, ident_raw[:])
-        nc.scalar.activation(ident[:], ident_raw[:], RELU)
         for plane in [xs] + w1sc + [w2sc, w1ssc, w2ssc]:
             nc.vector.memset(plane[:].bitcast(I32), 0)
 
@@ -77,39 +77,44 @@ def tile_moe_shf_mlp_relu_kernel(
             nc.sync.dma_start(out=xw[s][:], in_=x_words[s].rearrange("p t d -> p (t d)").bitcast(I32))
 
         def load_w1_words(g):
-            lo, hi = GROUPS[g]
+            lo, hi = PAIRS[g]
             src = w1_words[lo:hi].bitcast(I32).rearrange("e s p c -> p (e s) c")
             nc.sync.dma_start(out=w1[g][:].bitcast(I32), in_=src)
 
         def load_w1_scales(j):
             load_scale_rows(nc.sync, w1sc[j][:], w1_scales[j * RUN:(j + 1) * RUN].rearrange("e s b i -> (e s) b i"))
 
+        nc.scalar.activation(ident[:], ident_raw[:], RELU)
         load_x_words(0)
         load_scale_rows(nc.sync, xs[:], x_scales)
         nc.sync.dma_start(offs_sb[:], offs)
         load_x_words(1)
+        nc.sync.dma_start(out=gate_cols[:], in_=gate[:, 0, :].rearrange("r (p c) -> p r c", p=P))
         load_w1_words(0)
         load_w1_scales(0)
         load_w1_words(1)
         load_w1_words(2)
         load_w1_scales(1)
         load_w1_words(3)
-        for r, pos in enumerate((pos1, pos2, pos3)):
-            nc.sync.dma_start(pos_sb[r][:], pos)
         load_w1_words(4)
         load_w1_scales(2)
-        load_scale_rows(nc.sync, w2sc[:], w2_scales.rearrange("e s b n -> (e s) b n"))
         load_w1_words(5)
-        load_w1_words(6)
+        load_scale_rows(nc.sync, w2sc[:], w2_scales.rearrange("e s b n -> (e s) b n"))
         nc.sync.dma_start(out=w2[:].bitcast(I32), in_=w2_words.bitcast(I32).rearrange("e s p c -> p (e s) c"))
+        for r, pos in enumerate((pos1, pos2, pos3)):
+            nc.sync.dma_start(pos_sb[r][:], pos)
         nc.sync.dma_start(out=w1s[:], in_=w1s_words.rearrange("s p l d -> p s (l d)").bitcast(I32))
         load_scale_rows(nc.sync, w1ssc[:], w1s_scales)
-        nc.sync.dma_start(out=gate_first[:], in_=gate[0])
-        nc.sync.dma_start(out=gate_rest[:], in_=gate[1:TOP].rearrange("r p t -> p r t"))
         nc.sync.dma_start(out=w2s[:], in_=w2s_words[0].rearrange("p n d -> p (n d)").bitcast(I32))
         load_scale_rows(nc.sync, w2ssc[:], w2s_scales)
 
-        for lo, hi in GROUPS:
+        for r in range(TOP):
+            spread = banks[5 + r][:].rearrange("n (c p) -> n c p", p=P)
+            for c in range(T // P):
+                nc.tensor.transpose(spread[:, c, :], gate_cols[:, r, c:c + 1].to_broadcast([P, P]), ident[:])
+            nc.scalar.copy(gates[r][:].rearrange("n (p c) -> n p c", p=P), spread.rearrange("n c p -> n p c"))
+
+        for lo, hi in GATHERS:
             cols = slice(lo * C, hi * C)
             entries = offs_sb[:, lo * C // 16:hi * C // 16]
             nc.vector.tensor_copy(slot_words[0][:, cols], xw[0][:].bitcast(U32).indirect(entries))
@@ -126,83 +131,77 @@ def tile_moe_shf_mlp_relu_kernel(
                 h.rearrange("p (v m d) -> p v m d", v=2, d=2),
                 bank[:].rearrange("p (m v d) -> p v m d", v=2, d=2), RELU)
 
-        def first_layer(g):
-            lo, hi = GROUPS[g]
-            hidden[g] = sb("h%d" % g, [P, hi - lo, H], BF16)
-            for e in range(lo, hi):
-                bank = banks[e % 4]
-                for s in range(PASSES):
-                    w_at = ((e % RUN) * PASSES + s) * H
-                    nc.tensor.matmul_mx(
-                        out=bank[:], lhsT=slot_words[s][:, e * C:(e + 1) * C].bitcast(FP8X4),
-                        lhsT_scale=slot_scales[s][:, e * C:(e + 1) * C],
-                        rhs=w1[g][:, (e - lo) * PASSES + s, :].bitcast(FP4X4),
-                        rhs_scale=w1sc[e // RUN][:, w_at:w_at + H],
-                        start=(s == 0), stop=(s == PASSES - 1))
-                relu_out(hidden[g][:, e - lo, :], bank)
+        def first_layer(e):
+            hidden[e] = sb("h%d" % e, [P, H], BF16)
+            bank = banks[e % 4]
+            for s in range(PASSES):
+                w_at = ((e % RUN) * PASSES + s) * H
+                nc.tensor.matmul_mx(
+                    out=bank[:], lhsT=slot_words[s][:, e * C:(e + 1) * C].bitcast(FP8X4),
+                    lhsT_scale=slot_scales[s][:, e * C:(e + 1) * C],
+                    rhs=w1[e // 2][:, (e % 2) * PASSES + s, :].bitcast(FP4X4),
+                    rhs_scale=w1sc[e // RUN][:, w_at:w_at + H],
+                    start=(s == 0), stop=(s == PASSES - 1))
+            relu_out(hidden[e][:], bank)
 
-        def first_layer_shared(j):
-            key = "s%d" % j
-            hidden[key] = sb("h" + key, [P, 2, H], BF16)
-            for u in range(2):
-                bank = banks[2 * j + u]
-                t0 = (2 * j + u) * C
-                for s in range(PASSES):
-                    nc.tensor.matmul_mx(
-                        out=bank[:], lhsT=xw[s][:, t0:t0 + C].bitcast(FP8X4),
-                        lhsT_scale=xs[:, s * T + t0:s * T + t0 + C],
-                        rhs=w1s[:, s, :].bitcast(FP8X4), rhs_scale=w1ssc[:, s * H:(s + 1) * H],
-                        start=(s == 0), stop=(s == PASSES - 1))
-                relu_out(hidden[key][:, u, :], bank)
+        def first_layer_shared(b, bank):
+            key = "s%d" % b
+            hidden[key] = sb("h" + key, [P, H], BF16)
+            t0 = b * C
+            for s in range(PASSES):
+                nc.tensor.matmul_mx(
+                    out=bank[:], lhsT=xw[s][:, t0:t0 + C].bitcast(FP8X4),
+                    lhsT_scale=xs[:, s * T + t0:s * T + t0 + C],
+                    rhs=w1s[:, s, :].bitcast(FP8X4), rhs_scale=w1ssc[:, s * H:(s + 1) * H],
+                    start=(s == 0), stop=(s == PASSES - 1))
+            relu_out(hidden[key][:], bank)
 
-        def turn(key, bank, copy):
-            n = hidden[key].shape[1]
+        def turn(name, keys, bank):
+            n = len(keys)
             view = bank[:].rearrange("p (u v j) -> p u v j", u=2, v=2)
-            for u in range(n):
-                pairs = hidden[key][:, u, :].bitcast(F32)
+            for u in reversed(range(n)):
+                pairs = hidden[keys[u]][:].bitcast(F32)
                 for v in range(2):
                     nc.tensor.transpose(view[:, u, v, :], pairs[:, v * P:(v + 1) * P], ident[:])
-            dst = sb("ht%s" % key, [P, n * C * 4], BF16)
-            copy(dst[:].bitcast(F32).rearrange("p (u j v) -> p u j v", u=n, v=2),
-                 view[:, 0:n].rearrange("p u v j -> p u j v"))
-            grouped[key] = dst
+            dst = sb("ht%s" % name, [P, n * C * 4], BF16)
+            nc.scalar.copy(dst[:].bitcast(F32).rearrange("p (u j v) -> p u j v", u=n, v=2),
+                           view[:, 0:n].rearrange("p u v j -> p u j v"))
+            grouped[name] = dst
 
-        def quantise(key):
-            n = hidden[key].shape[1] * C
-            codes = sb("hq%s" % key, [P, n], U32)
-            scales = sb("hsc%s" % key, [P, n], U8)
-            nc.vector.quantize_mx(out=codes[:].bitcast(FP8X4), scales=scales[:], in_=grouped[key][:])
-            quantised[key] = (codes, scales)
+        def quantise(name):
+            n = grouped[name].shape[1] // 4
+            codes = sb("hq%s" % name, [P, n], U32)
+            scales = sb("hsc%s" % name, [P, n], U8)
+            nc.vector.quantize_mx(out=codes[:].bitcast(FP8X4), scales=scales[:], in_=grouped[name][:])
+            quantised[name] = (codes, scales)
 
-        def second_layer(gs, bank, copy):
-            first = GROUPS[gs[0]][0]
-            for g in gs:
+        def second_layer(first, end, bank, copy):
+            for e in range(first, end):
+                g = (e + 1) // 2
                 codes, scales = quantised[g]
-                lo, hi = GROUPS[g]
-                for e in range(lo, hi):
-                    cols = slice((e - lo) * C, (e - lo + 1) * C)
-                    nc.tensor.matmul_mx(
-                        out=bank[:, (e - first) * C:(e - first + 1) * C],
-                        lhsT=w2[:, e, :].bitcast(FP4X4), lhsT_scale=w2sc[:, e * N:(e + 1) * N],
-                        rhs=codes[:, cols].bitcast(FP8X4), rhs_scale=scales[:, cols], start=True, stop=True)
-            end = GROUPS[gs[-1]][1]
+                u = e - TURNS[g][0]
+                cols = slice(u * C, (u + 1) * C)
+                nc.tensor.matmul_mx(
+                    out=bank[:, (e - first) * C:(e - first + 1) * C],
+                    lhsT=w2[:, e, :].bitcast(FP4X4), lhsT_scale=w2sc[:, e * N:(e + 1) * N],
+                    rhs=codes[:, cols].bitcast(FP8X4), rhs_scale=scales[:, cols], start=True, stop=True)
             copy(y_slots[:, first * C:end * C], bank[:, 0:(end - first) * C])
 
-        first_layer(0)
-        for g in range(1, len(GROUPS)):
-            first_layer(g)
-            turn(g - 1, banks[4 + g % 2], nc.scalar.copy)
-        turn(len(GROUPS) - 1, banks[4 + len(GROUPS) % 2], nc.scalar.copy)
-        for g in range(len(GROUPS)):
+        for g, (lo, hi) in enumerate(PAIRS):
+            first_layer(lo)
+            first_layer(lo + 1)
+            turn(g, list(range(*TURNS[g])), banks[4 + g % 2])
+        turn(len(PAIRS), [E - 1], banks[4 + len(PAIRS) % 2])
+        for g in range(len(TURNS)):
             quantise(g)
-        second_layer([0, 1], banks[6], nc.scalar.copy)
-        second_layer([2, 3], banks[7], nc.vector.tensor_copy)
-        second_layer([4, 5], banks[0], nc.scalar.copy)
-        second_layer([6], banks[1], nc.vector.tensor_copy)
+        second_layer(0, 4, banks[6], nc.scalar.copy)
+        second_layer(4, 8, banks[7], nc.vector.tensor_copy)
+        second_layer(8, 11, banks[0], nc.scalar.copy)
+        second_layer(11, 12, banks[1], nc.vector.tensor_copy)
+        for b in range(4):
+            first_layer_shared(b, banks[2 + b])
         for j in range(2):
-            first_layer_shared(j)
-        for j in range(2):
-            turn("s%d" % j, banks[4 + j], nc.scalar.copy)
+            turn("s%d" % j, ["s%d" % (2 * j), "s%d" % (2 * j + 1)], banks[6 + j])
 
         terms = [sb("term%d" % r, [P, T], F32) for r in range(TOP)]
         sums = [sb("sum_two", [P, T], F32), grouped["s1"][:].bitcast(F32), sb("result", [P, T], F32)]
@@ -212,16 +211,18 @@ def tile_moe_shf_mlp_relu_kernel(
             quantise("s%d" % j)
             codes, scales = quantised["s%d" % j]
             nc.tensor.matmul_mx(
-                out=banks[6 + j][:, 0:half], lhsT=w2s[:].bitcast(FP8X4), lhsT_scale=w2ssc[:],
+                out=banks[j][:, 0:half], lhsT=w2s[:].bitcast(FP8X4), lhsT_scale=w2ssc[:],
                 rhs=codes[:].bitcast(FP8X4), rhs_scale=scales[:], start=True, stop=True)
 
         for r in range(TOP):
-            nc.vector.tensor_tensor(terms[r][:], y_slots[:].indirect(pos_sb[r][:]), gates[r], MULT)
+            nc.vector.tensor_tensor(terms[r][:], y_slots[:].indirect(pos_sb[r][:]), gates[r][:], MULT)
         nc.vector.tensor_tensor(sums[0][:], terms[0][:], terms[1][:], ADD)
         shared_second_layer(0)
         shared_second_layer(1)
-        nc.vector.tensor_tensor(sums[1], sums[0][:], terms[2][:], ADD)
         for j in range(2):
             cols = slice(j * half, (j + 1) * half)
-            nc.vector.tensor_tensor(sums[2][:, cols], sums[1][:, cols], banks[6 + j][:, 0:half], ADD)
+            nc.vector.tensor_tensor(sums[1][:, cols], sums[0][:, cols], terms[2][:, cols], ADD)
+        for j in range(2):
+            cols = slice(j * half, (j + 1) * half)
+            nc.vector.tensor_tensor(sums[2][:, cols], sums[1][:, cols], banks[j][:, 0:half], ADD)
             nc.sync.dma_start(out=out[:, cols], in_=sums[2][:, cols])

@@ -22,18 +22,22 @@ RELU = mybir.ActivationFunctionType.Relu
 MULT = mybir.AluOpType.mult
 ADD = mybir.AluOpType.add
 
-PAIRS = [(e, e + 2) for e in range(0, E, 2)]
-GATHERS = PAIRS[:-1] + [(E - 2, E - 1), (E - 1, E)]
+GROUPS = [(e, e + 2) for e in range(0, E - 2, 2)] + [(E - 2, E - 1), (E - 1, E)]
 TURNS = [(0, 1)] + [(e, e + 2) for e in range(1, E - 1, 2)] + [(E - 1, E)]
+VECTOR_TURNS = range(3, len(TURNS) - 1)
 RUN = 4
+BYTE_GATHER = 384
+HALF = E // 2
+W2_SPLIT = 8
+ZERO_WORDS = 32
 
 
-def load_scale_rows(queue, plane, rows):
-    blocks = rows.shape[0]
-    src = rows.bitcast(I32).rearrange("b (q r) w -> r q b w", r=4)
-    dst = plane.bitcast(I32).rearrange("p (b w) -> p b w", b=blocks)
+def load_scale_rows(nc, plane, rows):
+    sets = rows.shape[0]
+    src = rows.bitcast(I32).rearrange("g (q r) w -> r q g w", r=4)
+    dst = plane.bitcast(I32).rearrange("p (g w) -> p g w", g=sets)
     for r in range(4):
-        queue.dma_start(out=dst[r:P:32], in_=src[r])
+        nc.sync.dma_start(out=dst[r:P:32], in_=src[r])
 
 
 def tile_moe_shf_mlp_relu_kernel(
@@ -50,63 +54,91 @@ def tile_moe_shf_mlp_relu_kernel(
 
         offs_sb = keep.tile([P, SLOTS // 16], U16, name="offs_sb")
         pos_sb = [keep.tile([P, T // 16], U16, name="pos%d_sb" % r) for r in range(TOP)]
-        xw = [sb("xw%d" % s, [P, T], I32) for s in range(PASSES)]
-        xs = sb("xs", [P, PASSES * T], U8)
-        w1 = [sb("w1_%d" % lo, [P, (hi - lo) * PASSES, 2 * H], U8) for lo, hi in PAIRS]
-        w1sc = [sb("w1sc_%d" % j, [P, RUN * PASSES * H], U8) for j in range(E // RUN)]
-        w2 = sb("w2", [P, E, 2 * N], U8)
-        w2sc = sb("w2sc", [P, E * N], U8)
-        w1s = sb("w1s", [P, PASSES, H], I32)
+        xw_both = sb("xw", [P, PASSES * T], I32)
+        xw = [xw_both[:, s * T:(s + 1) * T] for s in range(PASSES)]
+        xs = sb("xs", [P, T], U8)
+        w1 = [sb("w1_%d" % lo, [P, (hi - lo) * PASSES, 2 * H], U8) for lo, hi in GROUPS]
+        w1s = sb("w1s", [P, PASSES * H * 4], U8)
         w1ssc = sb("w1ssc", [P, PASSES * H], U8)
-        w2s = sb("w2s", [P, N], I32)
+        w1sc = [sb("w1sc_%d" % j, [P, RUN * PASSES * H], U8) for j in range(E // RUN)]
+        w2sc = sb("w2sc", [P, E * N], U8)
         w2ssc = sb("w2ssc", [P, N], U8)
+        w2_parts = [(0, W2_SPLIT), (W2_SPLIT, E)]
+        w2 = [sb("w2_%d" % lo, [P, hi - lo, 2 * N], U8) for lo, hi in w2_parts]
+        w2s = sb("w2s", [P, N], I32)
         gate_cols = sb("gate_cols", [P, TOP, T // P], F32)
         gates = [sb("gate%d" % r, [P, T], F32) for r in range(TOP)]
         ident_raw = sb("ident_raw", [P, P], F32)
         ident = sb("ident", [P, P], F32)
         y_slots = sb("y_slots", [P, SLOTS], F32)
         slot_words = [sb("slot_words%d" % s, [P, SLOTS], U32) for s in range(PASSES)]
-        slot_scales = [sb("slot_scales%d" % s, [P, SLOTS], U8) for s in range(PASSES)]
+        slot_scales = [[sb("slot_scales%d_%d" % (j, s), [P, HALF * C], U8) for s in range(PASSES)] for j in range(2)]
         banks = [psum.tile([P, H], F32, name="bank%d" % b) for b in range(8)]
 
         make_identity(nc, ident_raw[:])
-        for plane in [xs] + w1sc + [w2sc, w1ssc, w2ssc]:
-            nc.vector.memset(plane[:].bitcast(I32), 0)
-
-        def load_x_words(s):
-            nc.sync.dma_start(out=xw[s][:], in_=x_words[s].rearrange("p t d -> p (t d)").bitcast(I32))
+        zero = sb("zero", [P, ZERO_WORDS], I32)
+        nc.vector.memset(xs[:].bitcast(I32), 0)
+        nc.vector.memset(zero[:], 0)
+        for plane in w1sc + [w2sc, w2ssc, w1ssc]:
+            words = plane[:].bitcast(I32).rearrange("p (a b) -> p a b", b=ZERO_WORDS)
+            nc.vector.tensor_copy(words, zero[:].unsqueeze(1).to_broadcast(list(words.shape)))
+        for j in range(2):
+            nc.vector.memset(slot_scales[j][1][:].bitcast(I32), 0)
 
         def load_w1_words(g):
-            lo, hi = PAIRS[g]
+            lo, hi = GROUPS[g]
             src = w1_words[lo:hi].bitcast(I32).rearrange("e s p c -> p (e s) c")
             nc.sync.dma_start(out=w1[g][:].bitcast(I32), in_=src)
 
         def load_w1_scales(j):
-            load_scale_rows(nc.sync, w1sc[j][:], w1_scales[j * RUN:(j + 1) * RUN].rearrange("e s b i -> (e s) b i"))
+            load_scale_rows(nc, w1sc[j][:], w1_scales[j * RUN:(j + 1) * RUN].rearrange("e s b i -> (e s) b i"))
+
+        def gather_scales(j):
+            both, lifted = slot_scales[j]
+            for lo in range(0, HALF * C, BYTE_GATHER):
+                first = j * HALF * C + lo
+                entries = offs_sb[:, first // 16:(first + BYTE_GATHER) // 16]
+                nc.vector.tensor_copy(both[:, lo:lo + BYTE_GATHER], xs[:].indirect(entries))
+            nc.sync.dma_start(out=lifted[0:P - 16, :].bitcast(I32), in_=both[4:P - 12, :].bitcast(I32))
+
+        def gather_words(g):
+            lo, hi = GROUPS[g]
+            entries = offs_sb[:, lo * C // 16:hi * C // 16]
+            for s in range(PASSES):
+                nc.vector.tensor_copy(slot_words[s][:, lo * C:hi * C], xw[s].bitcast(U32).indirect(entries))
 
         nc.scalar.activation(ident[:], ident_raw[:], RELU)
-        load_x_words(0)
-        load_scale_rows(nc.sync, xs[:], x_scales)
+
+        nc.sync.dma_start(out=xw_both[:].rearrange("p (s t) -> p s t", s=PASSES),
+                          in_=x_words.rearrange("s p t d -> p s (t d)").bitcast(I32))
+        for q in range(4):
+            nc.sync.dma_start(out=xs[32 * q:32 * q + 8, :].bitcast(I32), in_=x_scales[:, 4 * q:4 * q + 4, :].bitcast(I32))
         nc.sync.dma_start(offs_sb[:], offs)
-        load_x_words(1)
         nc.sync.dma_start(out=gate_cols[:], in_=gate[:, 0, :].rearrange("r (p c) -> p r c", p=P))
         load_w1_words(0)
-        load_w1_scales(0)
         load_w1_words(1)
+        load_w1_scales(0)
+        gather_scales(0)
+        gather_words(0)
+        gather_words(1)
         load_w1_words(2)
-        load_w1_scales(1)
         load_w1_words(3)
-        load_w1_words(4)
+        load_w1_scales(1)
+        gather_scales(1)
         load_w1_scales(2)
-        load_w1_words(5)
-        load_scale_rows(nc.sync, w2sc[:], w2_scales.rearrange("e s b n -> (e s) b n"))
-        nc.sync.dma_start(out=w2[:].bitcast(I32), in_=w2_words.bitcast(I32).rearrange("e s p c -> p (e s) c"))
+        for g in range(4, len(GROUPS)):
+            load_w1_words(g)
+        load_scale_rows(nc, w2sc[:], w2_scales.rearrange("e s b n -> (e s) b n"))
+        for j, (lo, hi) in enumerate(w2_parts):
+            nc.sync.dma_start(out=w2[j][:].bitcast(I32),
+                              in_=w2_words[lo:hi].bitcast(I32).rearrange("e s p c -> p (e s) c"))
+        nc.sync.dma_start(out=w1s[:].bitcast(I32).rearrange("p (s l) -> p s l", s=PASSES),
+                          in_=w1s_words.rearrange("s p l d -> p s (l d)").bitcast(I32))
+        load_scale_rows(nc, w1ssc[:], w1s_scales)
         for r, pos in enumerate((pos1, pos2, pos3)):
             nc.sync.dma_start(pos_sb[r][:], pos)
-        nc.sync.dma_start(out=w1s[:], in_=w1s_words.rearrange("s p l d -> p s (l d)").bitcast(I32))
-        load_scale_rows(nc.sync, w1ssc[:], w1s_scales)
         nc.sync.dma_start(out=w2s[:], in_=w2s_words[0].rearrange("p n d -> p (n d)").bitcast(I32))
-        load_scale_rows(nc.sync, w2ssc[:], w2s_scales)
+        load_scale_rows(nc, w2ssc[:], w2s_scales)
 
         for r in range(TOP):
             spread = banks[5 + r][:].rearrange("n (c p) -> n c p", p=P)
@@ -114,13 +146,8 @@ def tile_moe_shf_mlp_relu_kernel(
                 nc.tensor.transpose(spread[:, c, :], gate_cols[:, r, c:c + 1].to_broadcast([P, P]), ident[:])
             nc.scalar.copy(gates[r][:].rearrange("n (p c) -> n p c", p=P), spread.rearrange("n c p -> n p c"))
 
-        for lo, hi in GATHERS:
-            cols = slice(lo * C, hi * C)
-            entries = offs_sb[:, lo * C // 16:hi * C // 16]
-            nc.vector.tensor_copy(slot_words[0][:, cols], xw[0][:].bitcast(U32).indirect(entries))
-            for s in range(PASSES):
-                nc.vector.tensor_copy(slot_scales[s][:, cols], xs[:, s * T:(s + 1) * T].indirect(entries))
-            nc.vector.tensor_copy(slot_words[1][:, cols], xw[1][:].bitcast(U32).indirect(entries))
+        for g in range(2, len(GROUPS)):
+            gather_words(g)
 
         hidden = {}
         grouped = {}
@@ -133,14 +160,15 @@ def tile_moe_shf_mlp_relu_kernel(
 
         def first_layer(e):
             hidden[e] = sb("h%d" % e, [P, H], BF16)
-            bank = banks[e % 4]
+            bank = banks[e % RUN]
+            g = max(g for g, (lo, hi) in enumerate(GROUPS) if lo <= e)
             for s in range(PASSES):
-                w_at = ((e % RUN) * PASSES + s) * H
+                plane_at = ((e % RUN) * PASSES + s) * H
                 nc.tensor.matmul_mx(
                     out=bank[:], lhsT=slot_words[s][:, e * C:(e + 1) * C].bitcast(FP8X4),
-                    lhsT_scale=slot_scales[s][:, e * C:(e + 1) * C],
-                    rhs=w1[e // 2][:, (e % 2) * PASSES + s, :].bitcast(FP4X4),
-                    rhs_scale=w1sc[e // RUN][:, w_at:w_at + H],
+                    lhsT_scale=slot_scales[e // HALF][s][:, e % HALF * C:(e % HALF + 1) * C],
+                    rhs=w1[g][:, (e - GROUPS[g][0]) * PASSES + s, :].bitcast(FP4X4),
+                    rhs_scale=w1sc[e // RUN][:, plane_at:plane_at + H],
                     start=(s == 0), stop=(s == PASSES - 1))
             relu_out(hidden[e][:], bank)
 
@@ -151,12 +179,12 @@ def tile_moe_shf_mlp_relu_kernel(
             for s in range(PASSES):
                 nc.tensor.matmul_mx(
                     out=bank[:], lhsT=xw[s][:, t0:t0 + C].bitcast(FP8X4),
-                    lhsT_scale=xs[:, s * T + t0:s * T + t0 + C],
-                    rhs=w1s[:, s, :].bitcast(FP8X4), rhs_scale=w1ssc[:, s * H:(s + 1) * H],
+                    lhsT_scale=xs[4 * s:P, t0:t0 + C],
+                    rhs=w1s[:, s * H * 4:(s + 1) * H * 4].bitcast(FP8X4), rhs_scale=w1ssc[:, s * H:(s + 1) * H],
                     start=(s == 0), stop=(s == PASSES - 1))
             relu_out(hidden[key][:], bank)
 
-        def turn(name, keys, bank):
+        def turn(name, keys, bank, copy):
             n = len(keys)
             view = bank[:].rearrange("p (u v j) -> p u v j", u=2, v=2)
             for u in reversed(range(n)):
@@ -164,8 +192,8 @@ def tile_moe_shf_mlp_relu_kernel(
                 for v in range(2):
                     nc.tensor.transpose(view[:, u, v, :], pairs[:, v * P:(v + 1) * P], ident[:])
             dst = sb("ht%s" % name, [P, n * C * 4], BF16)
-            nc.scalar.copy(dst[:].bitcast(F32).rearrange("p (u j v) -> p u j v", u=n, v=2),
-                           view[:, 0:n].rearrange("p u v j -> p u j v"))
+            copy(dst[:].bitcast(F32).rearrange("p (u j v) -> p u j v", u=n, v=2),
+                 view[:, 0:n].rearrange("p u v j -> p u j v"))
             grouped[name] = dst
 
         def quantise(name):
@@ -183,46 +211,55 @@ def tile_moe_shf_mlp_relu_kernel(
                 cols = slice(u * C, (u + 1) * C)
                 nc.tensor.matmul_mx(
                     out=bank[:, (e - first) * C:(e - first + 1) * C],
-                    lhsT=w2[:, e, :].bitcast(FP4X4), lhsT_scale=w2sc[:, e * N:(e + 1) * N],
+                    lhsT=w2[e // W2_SPLIT][:, e % W2_SPLIT, :].bitcast(FP4X4), lhsT_scale=w2sc[:, e * N:(e + 1) * N],
                     rhs=codes[:, cols].bitcast(FP8X4), rhs_scale=scales[:, cols], start=True, stop=True)
             copy(y_slots[:, first * C:end * C], bank[:, 0:(end - first) * C])
 
-        for g, (lo, hi) in enumerate(PAIRS):
-            first_layer(lo)
-            first_layer(lo + 1)
-            turn(g, list(range(*TURNS[g])), banks[4 + g % 2])
-        turn(len(PAIRS), [E - 1], banks[4 + len(PAIRS) % 2])
+        def turn_routed(g):
+            bank = banks[4 + g % 2] if g < len(TURNS) - 2 else banks[1 + g]
+            turn(g, list(range(*TURNS[g])), bank, nc.vector.tensor_copy if g in VECTOR_TURNS else nc.scalar.copy)
+
+        for lo in range(0, E, RUN):
+            for e in range(lo, lo + RUN - 1):
+                first_layer(e)
+            turn_routed(lo // 2)
+            first_layer(lo + RUN - 1)
+            turn_routed(lo // 2 + 1)
+        turn_routed(len(TURNS) - 1)
         for g in range(len(TURNS)):
             quantise(g)
-        second_layer(0, 4, banks[6], nc.scalar.copy)
-        second_layer(4, 8, banks[7], nc.vector.tensor_copy)
-        second_layer(8, 11, banks[0], nc.scalar.copy)
-        second_layer(11, 12, banks[1], nc.vector.tensor_copy)
-        for b in range(4):
-            first_layer_shared(b, banks[2 + b])
+        second_layer(0, 4, banks[0], nc.scalar.copy)
+        second_layer(4, 8, banks[1], nc.vector.tensor_copy)
+        second_layer(8, E - 1, banks[2], nc.scalar.copy)
+        second_layer(E - 1, E, banks[3], nc.vector.tensor_copy)
+
+        for b in range(T // C):
+            first_layer_shared(b, banks[4 + b])
         for j in range(2):
-            turn("s%d" % j, ["s%d" % (2 * j), "s%d" % (2 * j + 1)], banks[6 + j])
+            turn("s%d" % j, ["s%d" % (2 * j), "s%d" % (2 * j + 1)], banks[j], nc.scalar.copy)
 
         terms = [sb("term%d" % r, [P, T], F32) for r in range(TOP)]
-        sums = [sb("sum_two", [P, T], F32), grouped["s1"][:].bitcast(F32), sb("result", [P, T], F32)]
+        sum_two = sb("sum_two", [P, T], F32)
+        sum_routed = grouped["s1"][:].bitcast(F32)
+        result = sb("result", [P, T], F32)
         half = T // 2
 
         def shared_second_layer(j):
             quantise("s%d" % j)
             codes, scales = quantised["s%d" % j]
             nc.tensor.matmul_mx(
-                out=banks[j][:, 0:half], lhsT=w2s[:].bitcast(FP8X4), lhsT_scale=w2ssc[:],
+                out=banks[2 + j][:, 0:half], lhsT=w2s[:].bitcast(FP8X4), lhsT_scale=w2ssc[:],
                 rhs=codes[:].bitcast(FP8X4), rhs_scale=scales[:], start=True, stop=True)
 
         for r in range(TOP):
             nc.vector.tensor_tensor(terms[r][:], y_slots[:].indirect(pos_sb[r][:]), gates[r][:], MULT)
-        nc.vector.tensor_tensor(sums[0][:], terms[0][:], terms[1][:], ADD)
+        nc.vector.tensor_tensor(sum_two[:], terms[0][:], terms[1][:], ADD)
         shared_second_layer(0)
         shared_second_layer(1)
         for j in range(2):
             cols = slice(j * half, (j + 1) * half)
-            nc.vector.tensor_tensor(sums[1][:, cols], sums[0][:, cols], terms[2][:, cols], ADD)
+            nc.vector.tensor_tensor(sum_routed[:, cols], sum_two[:, cols], terms[2][:, cols], ADD)
         for j in range(2):
             cols = slice(j * half, (j + 1) * half)
-            nc.vector.tensor_tensor(sums[2][:, cols], sums[1][:, cols], banks[j][:, 0:half], ADD)
-            nc.sync.dma_start(out=out[:, cols], in_=sums[2][:, cols])
+            nc.vector.tensor_tensor(result[:, cols], sum_routed[:, cols], banks[2 + j][:, 0:half], ADD)
+            nc.sync.dma_start(out=out[:, cols], in_=result[:, cols])

@@ -19,16 +19,19 @@ U8 = mybir.dt.uint8
 FP8X4 = mybir.dt.float8_e4m3fn_x4
 FP4X4 = mybir.dt.float4_e2m1fn_x4
 RELU = mybir.ActivationFunctionType.Relu
+COPY = mybir.ActivationFunctionType.Copy
 MULT = mybir.AluOpType.mult
 ADD = mybir.AluOpType.add
 
 GROUPS = [(e, e + 2) for e in range(0, E - 2, 2)] + [(E - 2, E - 1), (E - 1, E)]
-TURNS = [(0, 1)] + [(e, e + 2) for e in range(1, E - 1, 2)] + [(E - 1, E)]
+BLOCKS = T // C
+UNITS = BLOCKS + E
+TURNS = [(0, 1)] + [(u, u + 2) for u in range(1, UNITS - 1, 2)] + [(UNITS - 1, UNITS)]
 VECTOR_TURNS = range(3, len(TURNS) - 1)
 RUN = 4
 BYTE_GATHER = 384
 HALF = E // 2
-W2_SPLIT = 8
+W2_PARTS = [(0, 6), (6, 10), (10, E)]
 ZERO_WORDS = 32
 
 
@@ -63,8 +66,7 @@ def tile_moe_shf_mlp_relu_kernel(
         w1sc = [sb("w1sc_%d" % j, [P, RUN * PASSES * H], U8) for j in range(E // RUN)]
         w2sc = sb("w2sc", [P, E * N], U8)
         w2ssc = sb("w2ssc", [P, N], U8)
-        w2_parts = [(0, W2_SPLIT), (W2_SPLIT, E)]
-        w2 = [sb("w2_%d" % lo, [P, hi - lo, 2 * N], U8) for lo, hi in w2_parts]
+        w2 = [sb("w2_%d" % lo, [P, hi - lo, 2 * N], U8) for lo, hi in W2_PARTS]
         w2s = sb("w2s", [P, N], I32)
         gate_cols = sb("gate_cols", [P, TOP, T // P], F32)
         gates = [sb("gate%d" % r, [P, T], F32) for r in range(TOP)]
@@ -79,7 +81,7 @@ def tile_moe_shf_mlp_relu_kernel(
         zero = sb("zero", [P, ZERO_WORDS], I32)
         nc.vector.memset(xs[:].bitcast(I32), 0)
         nc.vector.memset(zero[:], 0)
-        for plane in w1sc + [w2sc, w2ssc, w1ssc]:
+        for plane in [w1ssc] + w1sc + [w2sc, w2ssc]:
             words = plane[:].bitcast(I32).rearrange("p (a b) -> p a b", b=ZERO_WORDS)
             nc.vector.tensor_copy(words, zero[:].unsqueeze(1).to_broadcast(list(words.shape)))
         for j in range(2):
@@ -109,12 +111,15 @@ def tile_moe_shf_mlp_relu_kernel(
 
         nc.scalar.activation(ident[:], ident_raw[:], RELU)
 
+        nc.sync.dma_start(out=gate_cols[:], in_=gate[:, 0, :].rearrange("r (p c) -> p r c", p=P))
         nc.sync.dma_start(out=xw_both[:].rearrange("p (s t) -> p s t", s=PASSES),
                           in_=x_words.rearrange("s p t d -> p s (t d)").bitcast(I32))
         for q in range(4):
             nc.sync.dma_start(out=xs[32 * q:32 * q + 8, :].bitcast(I32), in_=x_scales[:, 4 * q:4 * q + 4, :].bitcast(I32))
         nc.sync.dma_start(offs_sb[:], offs)
-        nc.sync.dma_start(out=gate_cols[:], in_=gate[:, 0, :].rearrange("r (p c) -> p r c", p=P))
+        nc.sync.dma_start(out=w1s[:].bitcast(I32).rearrange("p (s l) -> p s l", s=PASSES),
+                          in_=w1s_words.rearrange("s p l d -> p s (l d)").bitcast(I32))
+        load_scale_rows(nc, w1ssc[:], w1s_scales)
         load_w1_words(0)
         load_w1_words(1)
         load_w1_scales(0)
@@ -129,19 +134,16 @@ def tile_moe_shf_mlp_relu_kernel(
         for g in range(4, len(GROUPS)):
             load_w1_words(g)
         load_scale_rows(nc, w2sc[:], w2_scales.rearrange("e s b n -> (e s) b n"))
-        for j, (lo, hi) in enumerate(w2_parts):
+        for j, (lo, hi) in enumerate(W2_PARTS):
             nc.sync.dma_start(out=w2[j][:].bitcast(I32),
                               in_=w2_words[lo:hi].bitcast(I32).rearrange("e s p c -> p (e s) c"))
-        nc.sync.dma_start(out=w1s[:].bitcast(I32).rearrange("p (s l) -> p s l", s=PASSES),
-                          in_=w1s_words.rearrange("s p l d -> p s (l d)").bitcast(I32))
-        load_scale_rows(nc, w1ssc[:], w1s_scales)
         for r, pos in enumerate((pos1, pos2, pos3)):
             nc.sync.dma_start(pos_sb[r][:], pos)
         nc.sync.dma_start(out=w2s[:], in_=w2s_words[0].rearrange("p n d -> p (n d)").bitcast(I32))
         load_scale_rows(nc, w2ssc[:], w2s_scales)
 
         for r in range(TOP):
-            spread = banks[5 + r][:].rearrange("n (c p) -> n c p", p=P)
+            spread = banks[r][:].rearrange("n (c p) -> n c p", p=P)
             for c in range(T // P):
                 nc.tensor.transpose(spread[:, c, :], gate_cols[:, r, c:c + 1].to_broadcast([P, P]), ident[:])
             nc.scalar.copy(gates[r][:].rearrange("n (p c) -> n p c", p=P), spread.rearrange("n c p -> n p c"))
@@ -153,113 +155,113 @@ def tile_moe_shf_mlp_relu_kernel(
         grouped = {}
         quantised = {}
 
-        def relu_out(h, bank):
+        def first_bank(u):
+            return banks[u % TOP if u < BLOCKS else u % RUN]
+
+        def relu_out(u):
+            hidden[u] = sb("h%d" % u, [P, H], BF16)
             nc.scalar.activation(
-                h.rearrange("p (v m d) -> p v m d", v=2, d=2),
-                bank[:].rearrange("p (m v d) -> p v m d", v=2, d=2), RELU)
+                hidden[u][:].rearrange("p (v m d) -> p v m d", v=2, d=2),
+                first_bank(u)[:].rearrange("p (m v d) -> p v m d", v=2, d=2), RELU)
+
+        def first_layer_shared(b):
+            t0 = b * C
+            for s in range(PASSES):
+                nc.tensor.matmul_mx(
+                    out=first_bank(b)[:], lhsT=xw[s][:, t0:t0 + C].bitcast(FP8X4),
+                    lhsT_scale=xs[4 * s:P, t0:t0 + C],
+                    rhs=w1s[:, s * H * 4:(s + 1) * H * 4].bitcast(FP8X4), rhs_scale=w1ssc[:, s * H:(s + 1) * H],
+                    start=(s == 0), stop=(s == PASSES - 1))
+            relu_out(b)
 
         def first_layer(e):
-            hidden[e] = sb("h%d" % e, [P, H], BF16)
-            bank = banks[e % RUN]
             g = max(g for g, (lo, hi) in enumerate(GROUPS) if lo <= e)
             for s in range(PASSES):
                 plane_at = ((e % RUN) * PASSES + s) * H
                 nc.tensor.matmul_mx(
-                    out=bank[:], lhsT=slot_words[s][:, e * C:(e + 1) * C].bitcast(FP8X4),
+                    out=first_bank(BLOCKS + e)[:], lhsT=slot_words[s][:, e * C:(e + 1) * C].bitcast(FP8X4),
                     lhsT_scale=slot_scales[e // HALF][s][:, e % HALF * C:(e % HALF + 1) * C],
                     rhs=w1[g][:, (e - GROUPS[g][0]) * PASSES + s, :].bitcast(FP4X4),
                     rhs_scale=w1sc[e // RUN][:, plane_at:plane_at + H],
                     start=(s == 0), stop=(s == PASSES - 1))
-            relu_out(hidden[e][:], bank)
+            relu_out(BLOCKS + e)
 
-        def first_layer_shared(b, bank):
-            key = "s%d" % b
-            hidden[key] = sb("h" + key, [P, H], BF16)
-            t0 = b * C
-            for s in range(PASSES):
-                nc.tensor.matmul_mx(
-                    out=bank[:], lhsT=xw[s][:, t0:t0 + C].bitcast(FP8X4),
-                    lhsT_scale=xs[4 * s:P, t0:t0 + C],
-                    rhs=w1s[:, s * H * 4:(s + 1) * H * 4].bitcast(FP8X4), rhs_scale=w1ssc[:, s * H:(s + 1) * H],
-                    start=(s == 0), stop=(s == PASSES - 1))
-            relu_out(hidden[key][:], bank)
-
-        def turn(name, keys, bank, copy):
-            n = len(keys)
-            view = bank[:].rearrange("p (u v j) -> p u v j", u=2, v=2)
+        def turn(i):
+            lo, hi = TURNS[i]
+            n = hi - lo
+            view = banks[RUN + i % RUN][:].rearrange("p (u v j) -> p u v j", u=2, v=2)
             for u in reversed(range(n)):
-                pairs = hidden[keys[u]][:].bitcast(F32)
+                pairs = hidden[lo + u][:].bitcast(F32)
                 for v in range(2):
                     nc.tensor.transpose(view[:, u, v, :], pairs[:, v * P:(v + 1) * P], ident[:])
-            dst = sb("ht%s" % name, [P, n * C * 4], BF16)
-            copy(dst[:].bitcast(F32).rearrange("p (u j v) -> p u j v", u=n, v=2),
+            grouped[i] = sb("ht%d" % i, [P, n * C * 4], BF16)
+            copy = nc.vector.tensor_copy if i in VECTOR_TURNS else nc.scalar.copy
+            copy(grouped[i][:].bitcast(F32).rearrange("p (u j v) -> p u j v", u=n, v=2),
                  view[:, 0:n].rearrange("p u v j -> p u j v"))
-            grouped[name] = dst
 
-        def quantise(name):
-            n = grouped[name].shape[1] // 4
-            codes = sb("hq%s" % name, [P, n], U32)
-            scales = sb("hsc%s" % name, [P, n], U8)
-            nc.vector.quantize_mx(out=codes[:].bitcast(FP8X4), scales=scales[:], in_=grouped[name][:])
-            quantised[name] = (codes, scales)
+        def quantise(i):
+            lo, hi = TURNS[i]
+            codes = sb("hq%d" % i, [P, (hi - lo) * C], U32)
+            scales = sb("hsc%d" % i, [P, (hi - lo) * C], U8)
+            nc.vector.quantize_mx(out=codes[:].bitcast(FP8X4), scales=scales[:], in_=grouped[i][:])
+            for u in range(lo, hi):
+                cols = slice((u - lo) * C, (u - lo + 1) * C)
+                quantised[u] = (codes[:, cols].bitcast(FP8X4), scales[:, cols])
 
         def second_layer(first, end, bank, copy):
             for e in range(first, end):
-                g = (e + 1) // 2
-                codes, scales = quantised[g]
-                u = e - TURNS[g][0]
-                cols = slice(u * C, (u + 1) * C)
+                codes, scales = quantised[BLOCKS + e]
+                part = max(j for j, (lo, hi) in enumerate(W2_PARTS) if lo <= e)
                 nc.tensor.matmul_mx(
                     out=bank[:, (e - first) * C:(e - first + 1) * C],
-                    lhsT=w2[e // W2_SPLIT][:, e % W2_SPLIT, :].bitcast(FP4X4), lhsT_scale=w2sc[:, e * N:(e + 1) * N],
-                    rhs=codes[:, cols].bitcast(FP8X4), rhs_scale=scales[:, cols], start=True, stop=True)
+                    lhsT=w2[part][:, e - W2_PARTS[part][0], :].bitcast(FP4X4), lhsT_scale=w2sc[:, e * N:(e + 1) * N],
+                    rhs=codes, rhs_scale=scales, start=True, stop=True)
             copy(y_slots[:, first * C:end * C], bank[:, 0:(end - first) * C])
 
-        def turn_routed(g):
-            bank = banks[4 + g % 2] if g < len(TURNS) - 2 else banks[1 + g]
-            turn(g, list(range(*TURNS[g])), bank, nc.vector.tensor_copy if g in VECTOR_TURNS else nc.scalar.copy)
+        def first_layer_of(u):
+            if u < BLOCKS:
+                first_layer_shared(u)
+            else:
+                first_layer(u - BLOCKS)
 
-        for lo in range(0, E, RUN):
-            for e in range(lo, lo + RUN - 1):
-                first_layer(e)
-            turn_routed(lo // 2)
-            first_layer(lo + RUN - 1)
-            turn_routed(lo // 2 + 1)
-        turn_routed(len(TURNS) - 1)
-        for g in range(len(TURNS)):
-            quantise(g)
-        second_layer(0, 4, banks[0], nc.scalar.copy)
-        second_layer(4, 8, banks[1], nc.vector.tensor_copy)
-        second_layer(8, E - 1, banks[2], nc.scalar.copy)
-        second_layer(E - 1, E, banks[3], nc.vector.tensor_copy)
+        for lo in range(0, UNITS - RUN, RUN):
+            for u in range(lo, lo + RUN):
+                first_layer_of(u)
+            turn(lo // 2)
+            turn(lo // 2 + 1)
+        for u in range(UNITS - RUN, UNITS - 1):
+            first_layer_of(u)
+        turn(len(TURNS) - 3)
+        first_layer_of(UNITS - 1)
+        turn(len(TURNS) - 2)
+        turn(len(TURNS) - 1)
+        for i in range(len(TURNS)):
+            quantise(i)
+        second_layer(0, 3, banks[0], nc.scalar.copy)
+        second_layer(3, 6, banks[1], nc.vector.tensor_copy)
+        second_layer(6, 10, banks[2], nc.scalar.copy)
+        second_layer(10, E, banks[3], nc.vector.tensor_copy)
 
-        for b in range(T // C):
-            first_layer_shared(b, banks[4 + b])
-        for j in range(2):
-            turn("s%d" % j, ["s%d" % (2 * j), "s%d" % (2 * j + 1)], banks[j], nc.scalar.copy)
-
-        terms = [sb("term%d" % r, [P, T], F32) for r in range(TOP)]
-        sum_two = sb("sum_two", [P, T], F32)
-        sum_routed = grouped["s1"][:].bitcast(F32)
-        result = sb("result", [P, T], F32)
-        half = T // 2
-
-        def shared_second_layer(j):
-            quantise("s%d" % j)
-            codes, scales = quantised["s%d" % j]
+        shared = banks[RUN + 1]
+        for b in range(BLOCKS):
+            codes, scales = quantised[b]
             nc.tensor.matmul_mx(
-                out=banks[2 + j][:, 0:half], lhsT=w2s[:].bitcast(FP8X4), lhsT_scale=w2ssc[:],
-                rhs=codes[:].bitcast(FP8X4), rhs_scale=scales[:], start=True, stop=True)
+                out=shared[:, b * C:(b + 1) * C], lhsT=w2s[:].bitcast(FP8X4), lhsT_scale=w2ssc[:],
+                rhs=codes, rhs_scale=scales, start=True, stop=True)
 
-        for r in range(TOP):
-            nc.vector.tensor_tensor(terms[r][:], y_slots[:].indirect(pos_sb[r][:]), gates[r][:], MULT)
-        nc.vector.tensor_tensor(sum_two[:], terms[0][:], terms[1][:], ADD)
-        shared_second_layer(0)
-        shared_second_layer(1)
-        for j in range(2):
-            cols = slice(j * half, (j + 1) * half)
-            nc.vector.tensor_tensor(sum_routed[:, cols], sum_two[:, cols], terms[2][:, cols], ADD)
-        for j in range(2):
-            cols = slice(j * half, (j + 1) * half)
-            nc.vector.tensor_tensor(result[:, cols], sum_routed[:, cols], banks[2 + j][:, 0:half], ADD)
-            nc.sync.dma_start(out=out[:, cols], in_=result[:, cols])
+        picked = [sb("picked%d" % r, [P, T], F32) for r in range(1, TOP)]
+        terms = [sb("term%d" % r, [P, T], F32) for r in range(TOP)]
+        sums = [sb("sum%d" % r, [P, T], F32) for r in range(TOP)]
+        halves = [slice(0, T // 2), slice(T // 2, T)]
+        nc.vector.tensor_tensor(terms[0][:], y_slots[:].indirect(pos_sb[0][:]), gates[0][:], MULT)
+        for r in range(1, TOP):
+            nc.scalar.activation(picked[r - 1][:], y_slots[:].indirect(pos_sb[r][:]), COPY)
+        for r in range(1, TOP):
+            before = terms[0] if r == 1 else sums[r - 2]
+            for cols in halves:
+                nc.vector.tensor_tensor(terms[r][:, cols], picked[r - 1][:, cols], gates[r][:, cols], MULT)
+            for cols in halves:
+                nc.vector.tensor_tensor(sums[r - 1][:, cols], terms[r][:, cols], before[:, cols], ADD)
+        for cols in halves:
+            nc.vector.tensor_tensor(sums[TOP - 1][:, cols], sums[TOP - 2][:, cols], shared[:, cols], ADD)
+            nc.sync.dma_start(out=out[:, cols], in_=sums[TOP - 1][:, cols])

@@ -23,15 +23,16 @@ COPY = mybir.ActivationFunctionType.Copy
 MULT = mybir.AluOpType.mult
 ADD = mybir.AluOpType.add
 
-GROUPS = [(e, e + 2) for e in range(0, E - 2, 2)] + [(E - 2, E - 1), (E - 1, E)]
 BLOCKS = T // C
 UNITS = BLOCKS + E
-TURNS = [(0, 1)] + [(u, u + 2) for u in range(1, UNITS - 1, 2)] + [(UNITS - 1, UNITS)]
-VECTOR_TURNS = range(3, len(TURNS) - 1)
 RUN = 4
+GROUPS = [(e, e + 2) for e in range(0, E - 2, 2)] + [(E - 2, E - 1), (E - 1, E)]
+TURNS = [[u for u in turn if u >= 0] for lo in range(0, UNITS, RUN) for turn in ((lo + 2, lo - 1), (lo, lo + 1))]
+TURNS = TURNS + [[UNITS - 1]]
+VECTOR_TURNS = (1, 3, 5, 6)
 BYTE_GATHER = 384
-HALF = E // 2
-W2_PARTS = [(0, 6), (6, 10), (10, E)]
+BYTE_PARTS = [(0, RUN), (RUN, E)]
+W2_PARTS = [(0, 8), (8, E)]
 ZERO_WORDS = 32
 
 
@@ -57,24 +58,23 @@ def tile_moe_shf_mlp_relu_kernel(
 
         offs_sb = keep.tile([P, SLOTS // 16], U16, name="offs_sb")
         pos_sb = [keep.tile([P, T // 16], U16, name="pos%d_sb" % r) for r in range(TOP)]
-        xw_both = sb("xw", [P, PASSES * T], I32)
-        xw = [xw_both[:, s * T:(s + 1) * T] for s in range(PASSES)]
+        xw = sb("xw", [P, PASSES * T], I32)
         xs = sb("xs", [P, T], U8)
         w1 = [sb("w1_%d" % lo, [P, (hi - lo) * PASSES, 2 * H], U8) for lo, hi in GROUPS]
-        w1s = sb("w1s", [P, PASSES * H * 4], U8)
+        w1s = [sb("w1s%d" % s, [P, H * 4], U8) for s in range(PASSES)]
         w1ssc = sb("w1ssc", [P, PASSES * H], U8)
         w1sc = [sb("w1sc_%d" % j, [P, RUN * PASSES * H], U8) for j in range(E // RUN)]
         w2sc = sb("w2sc", [P, E * N], U8)
         w2ssc = sb("w2ssc", [P, N], U8)
         w2 = [sb("w2_%d" % lo, [P, hi - lo, 2 * N], U8) for lo, hi in W2_PARTS]
         w2s = sb("w2s", [P, N], I32)
-        gate_cols = sb("gate_cols", [P, TOP, T // P], F32)
         gates = [sb("gate%d" % r, [P, T], F32) for r in range(TOP)]
         ident_raw = sb("ident_raw", [P, P], F32)
         ident = sb("ident", [P, P], F32)
         y_slots = sb("y_slots", [P, SLOTS], F32)
         slot_words = [sb("slot_words%d" % s, [P, SLOTS], U32) for s in range(PASSES)]
-        slot_scales = [[sb("slot_scales%d_%d" % (j, s), [P, HALF * C], U8) for s in range(PASSES)] for j in range(2)]
+        slot_scales = [[sb("slot_scales%d_%d" % (lo, s), [P, (hi - lo) * C], U8) for s in range(PASSES)]
+                       for lo, hi in BYTE_PARTS]
         banks = [psum.tile([P, H], F32, name="bank%d" % b) for b in range(8)]
 
         make_identity(nc, ident_raw[:])
@@ -84,8 +84,16 @@ def tile_moe_shf_mlp_relu_kernel(
         for plane in [w1ssc] + w1sc + [w2sc, w2ssc]:
             words = plane[:].bitcast(I32).rearrange("p (a b) -> p a b", b=ZERO_WORDS)
             nc.vector.tensor_copy(words, zero[:].unsqueeze(1).to_broadcast(list(words.shape)))
-        for j in range(2):
-            nc.vector.memset(slot_scales[j][1][:].bitcast(I32), 0)
+        for both, lifted in slot_scales:
+            nc.vector.memset(lifted[:].bitcast(I32), 0)
+
+        def load_pass(dst, words, s):
+            nc.sync.dma_start(out=dst, in_=words[s].rearrange("p t d -> p (t d)").bitcast(I32))
+
+        def load_tokens(half):
+            cols = slice(half * T // 2, (half + 1) * T // 2)
+            nc.sync.dma_start(out=xw[:].rearrange("p (s t) -> p s t", s=PASSES)[:, :, cols],
+                              in_=x_words[:, :, cols, :].rearrange("s p t d -> p s (t d)").bitcast(I32))
 
         def load_w1_words(g):
             lo, hi = GROUPS[g]
@@ -96,40 +104,41 @@ def tile_moe_shf_mlp_relu_kernel(
             load_scale_rows(nc, w1sc[j][:], w1_scales[j * RUN:(j + 1) * RUN].rearrange("e s b i -> (e s) b i"))
 
         def gather_scales(j):
+            lo, hi = BYTE_PARTS[j]
+            for at in range(0, (hi - lo) * C, BYTE_GATHER):
+                end = min(at + BYTE_GATHER, (hi - lo) * C)
+                entries = offs_sb[:, (lo * C + at) // 16:(lo * C + end) // 16]
+                nc.vector.tensor_copy(slot_scales[j][0][:, at:end], xs[:].indirect(entries))
+
+        def lift_scales(j):
             both, lifted = slot_scales[j]
-            for lo in range(0, HALF * C, BYTE_GATHER):
-                first = j * HALF * C + lo
-                entries = offs_sb[:, first // 16:(first + BYTE_GATHER) // 16]
-                nc.vector.tensor_copy(both[:, lo:lo + BYTE_GATHER], xs[:].indirect(entries))
             nc.sync.dma_start(out=lifted[0:P - 16, :].bitcast(I32), in_=both[4:P - 12, :].bitcast(I32))
 
-        def gather_words(g):
-            lo, hi = GROUPS[g]
+        def gather_words(lo, hi):
             entries = offs_sb[:, lo * C // 16:hi * C // 16]
             for s in range(PASSES):
-                nc.vector.tensor_copy(slot_words[s][:, lo * C:hi * C], xw[s].bitcast(U32).indirect(entries))
+                nc.vector.tensor_copy(slot_words[s][:, lo * C:hi * C], xw[:, s * T:].bitcast(U32).indirect(entries))
 
         nc.scalar.activation(ident[:], ident_raw[:], RELU)
 
-        nc.sync.dma_start(out=gate_cols[:], in_=gate[:, 0, :].rearrange("r (p c) -> p r c", p=P))
-        nc.sync.dma_start(out=xw_both[:].rearrange("p (s t) -> p s t", s=PASSES),
-                          in_=x_words.rearrange("s p t d -> p s (t d)").bitcast(I32))
+        load_tokens(0)
+        nc.sync.dma_start(offs_sb[:], offs)
         for q in range(4):
             nc.sync.dma_start(out=xs[32 * q:32 * q + 8, :].bitcast(I32), in_=x_scales[:, 4 * q:4 * q + 4, :].bitcast(I32))
-        nc.sync.dma_start(offs_sb[:], offs)
-        nc.sync.dma_start(out=w1s[:].bitcast(I32).rearrange("p (s l) -> p s l", s=PASSES),
-                          in_=w1s_words.rearrange("s p l d -> p s (l d)").bitcast(I32))
+        load_pass(w1s[0][:].bitcast(I32), w1s_words, 0)
+        load_pass(w1s[1][:].bitcast(I32), w1s_words, 1)
         load_scale_rows(nc, w1ssc[:], w1s_scales)
-        load_w1_words(0)
-        load_w1_words(1)
-        load_w1_scales(0)
+        load_tokens(1)
         gather_scales(0)
-        gather_words(0)
-        gather_words(1)
+        gather_scales(1)
+        load_w1_scales(0)
+        load_w1_words(0)
+        lift_scales(0)
+        load_w1_words(1)
+        load_w1_scales(1)
+        lift_scales(1)
         load_w1_words(2)
         load_w1_words(3)
-        load_w1_scales(1)
-        gather_scales(1)
         load_w1_scales(2)
         for g in range(4, len(GROUPS)):
             load_w1_words(g)
@@ -139,73 +148,72 @@ def tile_moe_shf_mlp_relu_kernel(
                               in_=w2_words[lo:hi].bitcast(I32).rearrange("e s p c -> p (e s) c"))
         for r, pos in enumerate((pos1, pos2, pos3)):
             nc.sync.dma_start(pos_sb[r][:], pos)
+        nc.sync.dma_start(out=gates[0][:], in_=gate[0])
         nc.sync.dma_start(out=w2s[:], in_=w2s_words[0].rearrange("p n d -> p (n d)").bitcast(I32))
         load_scale_rows(nc, w2ssc[:], w2s_scales)
+        for r in range(1, TOP):
+            nc.sync.dma_start(out=gates[r][:], in_=gate[r])
 
-        for r in range(TOP):
-            spread = banks[r][:].rearrange("n (c p) -> n c p", p=P)
-            for c in range(T // P):
-                nc.tensor.transpose(spread[:, c, :], gate_cols[:, r, c:c + 1].to_broadcast([P, P]), ident[:])
-            nc.scalar.copy(gates[r][:].rearrange("n (p c) -> n p c", p=P), spread.rearrange("n c p -> n p c"))
+        for e in range(0, E, 2):
+            gather_words(e, e + 2)
 
-        for g in range(2, len(GROUPS)):
-            gather_words(g)
-
-        hidden = {}
+        hidden = [sb("h%d" % u, [P, H], BF16)[:] for u in range(UNITS)]
         grouped = {}
         quantised = {}
 
         def first_bank(u):
-            return banks[u % TOP if u < BLOCKS else u % RUN]
+            return banks[(2, 5, 7)[u // RUN % 3] if u % RUN == 2 else u % RUN]
+
+        def turn_bank(i):
+            if i == len(TURNS) - 1:
+                return banks[5]
+            return first_bank(i // 2 * RUN + 2) if i % 2 else banks[4 + 2 * (i // 2 % 2)]
 
         def relu_out(u):
-            hidden[u] = sb("h%d" % u, [P, H], BF16)
             nc.scalar.activation(
-                hidden[u][:].rearrange("p (v m d) -> p v m d", v=2, d=2),
+                hidden[u].rearrange("p (v m d) -> p v m d", v=2, d=2),
                 first_bank(u)[:].rearrange("p (m v d) -> p v m d", v=2, d=2), RELU)
 
-        def first_layer_shared(b):
+        def shared_pass(b, s):
             t0 = b * C
-            for s in range(PASSES):
-                nc.tensor.matmul_mx(
-                    out=first_bank(b)[:], lhsT=xw[s][:, t0:t0 + C].bitcast(FP8X4),
-                    lhsT_scale=xs[4 * s:P, t0:t0 + C],
-                    rhs=w1s[:, s * H * 4:(s + 1) * H * 4].bitcast(FP8X4), rhs_scale=w1ssc[:, s * H:(s + 1) * H],
-                    start=(s == 0), stop=(s == PASSES - 1))
-            relu_out(b)
+            nc.tensor.matmul_mx(
+                out=first_bank(b)[:], lhsT=xw[:, s * T + t0:s * T + t0 + C].bitcast(FP8X4),
+                lhsT_scale=xs[4 * s:P, t0:t0 + C],
+                rhs=w1s[s][:].bitcast(FP8X4), rhs_scale=w1ssc[:, s * H:(s + 1) * H],
+                start=(s == 0), stop=(s == PASSES - 1))
 
         def first_layer(e):
             g = max(g for g, (lo, hi) in enumerate(GROUPS) if lo <= e)
+            j = max(j for j, (lo, hi) in enumerate(BYTE_PARTS) if lo <= e)
+            at = (e - BYTE_PARTS[j][0]) * C
             for s in range(PASSES):
                 plane_at = ((e % RUN) * PASSES + s) * H
                 nc.tensor.matmul_mx(
                     out=first_bank(BLOCKS + e)[:], lhsT=slot_words[s][:, e * C:(e + 1) * C].bitcast(FP8X4),
-                    lhsT_scale=slot_scales[e // HALF][s][:, e % HALF * C:(e % HALF + 1) * C],
+                    lhsT_scale=slot_scales[j][s][:, at:at + C],
                     rhs=w1[g][:, (e - GROUPS[g][0]) * PASSES + s, :].bitcast(FP4X4),
                     rhs_scale=w1sc[e // RUN][:, plane_at:plane_at + H],
                     start=(s == 0), stop=(s == PASSES - 1))
             relu_out(BLOCKS + e)
 
         def turn(i):
-            lo, hi = TURNS[i]
-            n = hi - lo
-            view = banks[RUN + i % RUN][:].rearrange("p (u v j) -> p u v j", u=2, v=2)
-            for u in reversed(range(n)):
-                pairs = hidden[lo + u][:].bitcast(F32)
+            n = len(TURNS[i])
+            view = turn_bank(i)[:].rearrange("p (u v j) -> p u v j", u=2, v=2)
+            for k, u in enumerate(TURNS[i]):
+                pairs = hidden[u].bitcast(F32)
                 for v in range(2):
-                    nc.tensor.transpose(view[:, u, v, :], pairs[:, v * P:(v + 1) * P], ident[:])
+                    nc.tensor.transpose(view[:, k, v, :], pairs[:, v * P:(v + 1) * P], ident[:])
             grouped[i] = sb("ht%d" % i, [P, n * C * 4], BF16)
             copy = nc.vector.tensor_copy if i in VECTOR_TURNS else nc.scalar.copy
             copy(grouped[i][:].bitcast(F32).rearrange("p (u j v) -> p u j v", u=n, v=2),
                  view[:, 0:n].rearrange("p u v j -> p u j v"))
 
         def quantise(i):
-            lo, hi = TURNS[i]
-            codes = sb("hq%d" % i, [P, (hi - lo) * C], U32)
-            scales = sb("hsc%d" % i, [P, (hi - lo) * C], U8)
+            codes = sb("hq%d" % i, [P, len(TURNS[i]) * C], U32)
+            scales = sb("hsc%d" % i, [P, len(TURNS[i]) * C], U8)
             nc.vector.quantize_mx(out=codes[:].bitcast(FP8X4), scales=scales[:], in_=grouped[i][:])
-            for u in range(lo, hi):
-                cols = slice((u - lo) * C, (u - lo + 1) * C)
+            for k, u in enumerate(TURNS[i]):
+                cols = slice(k * C, (k + 1) * C)
                 quantised[u] = (codes[:, cols].bitcast(FP8X4), scales[:, cols])
 
         def second_layer(first, end, bank, copy):
@@ -218,31 +226,26 @@ def tile_moe_shf_mlp_relu_kernel(
                     rhs=codes, rhs_scale=scales, start=True, stop=True)
             copy(y_slots[:, first * C:end * C], bank[:, 0:(end - first) * C])
 
-        def first_layer_of(u):
-            if u < BLOCKS:
-                first_layer_shared(u)
-            else:
-                first_layer(u - BLOCKS)
-
-        for lo in range(0, UNITS - RUN, RUN):
-            for u in range(lo, lo + RUN):
-                first_layer_of(u)
-            turn(lo // 2)
-            turn(lo // 2 + 1)
-        for u in range(UNITS - RUN, UNITS - 1):
-            first_layer_of(u)
-        turn(len(TURNS) - 3)
-        first_layer_of(UNITS - 1)
-        turn(len(TURNS) - 2)
+        for b in range(BLOCKS):
+            for s in range(PASSES):
+                shared_pass(b, s)
+            relu_out(b)
+        turn(0)
+        turn(1)
+        for lo in range(0, E, RUN):
+            for e in range(lo, lo + RUN):
+                first_layer(e)
+            turn((BLOCKS + lo) // 2)
+            turn((BLOCKS + lo) // 2 + 1)
         turn(len(TURNS) - 1)
         for i in range(len(TURNS)):
             quantise(i)
-        second_layer(0, 3, banks[0], nc.scalar.copy)
-        second_layer(3, 6, banks[1], nc.vector.tensor_copy)
-        second_layer(6, 10, banks[2], nc.scalar.copy)
-        second_layer(10, E, banks[3], nc.vector.tensor_copy)
+        second_layer(0, 4, banks[0], nc.scalar.copy)
+        second_layer(4, 8, banks[1], nc.vector.tensor_copy)
+        second_layer(8, E - 1, banks[4], nc.scalar.copy)
+        second_layer(E - 1, E, banks[3], nc.vector.tensor_copy)
 
-        shared = banks[RUN + 1]
+        shared = banks[7]
         for b in range(BLOCKS):
             codes, scales = quantised[b]
             nc.tensor.matmul_mx(
@@ -256,12 +259,11 @@ def tile_moe_shf_mlp_relu_kernel(
         nc.vector.tensor_tensor(terms[0][:], y_slots[:].indirect(pos_sb[0][:]), gates[0][:], MULT)
         for r in range(1, TOP):
             nc.scalar.activation(picked[r - 1][:], y_slots[:].indirect(pos_sb[r][:]), COPY)
-        for r in range(1, TOP):
-            before = terms[0] if r == 1 else sums[r - 2]
-            for cols in halves:
-                nc.vector.tensor_tensor(terms[r][:, cols], picked[r - 1][:, cols], gates[r][:, cols], MULT)
-            for cols in halves:
-                nc.vector.tensor_tensor(sums[r - 1][:, cols], terms[r][:, cols], before[:, cols], ADD)
+        nc.vector.tensor_tensor(terms[1][:], picked[0][:], gates[1][:], MULT)
+        nc.vector.tensor_tensor(sums[0][:], terms[0][:], shared[:], ADD)
+        nc.vector.tensor_tensor(terms[2][:], picked[1][:], gates[2][:], MULT)
         for cols in halves:
-            nc.vector.tensor_tensor(sums[TOP - 1][:, cols], sums[TOP - 2][:, cols], shared[:, cols], ADD)
-            nc.sync.dma_start(out=out[:, cols], in_=sums[TOP - 1][:, cols])
+            nc.vector.tensor_tensor(sums[1][:, cols], sums[0][:, cols], terms[1][:, cols], ADD)
+        for cols in halves:
+            nc.vector.tensor_tensor(sums[2][:, cols], sums[1][:, cols], terms[2][:, cols], ADD)
+            nc.sync.dma_start(out=out[:, cols], in_=sums[2][:, cols])

@@ -54,7 +54,7 @@ def tile_moe_shf_mlp_relu_kernel(
         psum = ctx.enter_context(tc.psum_pool(name="psum", bufs=1))
 
         def sb(name, shape, dtype):
-            return keep.tile(shape, dtype, name=name, align_bytes=64)
+            return keep.tile(shape, dtype, name=name, align_bytes=256)
 
         offs_sb = keep.tile([P, SLOTS // 16], U16, name="offs_sb")
         pos_sb = [keep.tile([P, T // 16], U16, name="pos%d_sb" % r) for r in range(TOP)]
@@ -68,6 +68,7 @@ def tile_moe_shf_mlp_relu_kernel(
         w2ssc = sb("w2ssc", [P, N], U8)
         w2 = [sb("w2_%d" % lo, [P, hi - lo, 2 * N], U8) for lo, hi in W2_PARTS]
         w2s = sb("w2s", [P, N], I32)
+        gate_cols = sb("gate_cols", [P, TOP, T // P], F32)
         gates = [sb("gate%d" % r, [P, T], F32) for r in range(TOP)]
         ident_raw = sb("ident_raw", [P, P], F32)
         ident = sb("ident", [P, P], F32)
@@ -121,6 +122,7 @@ def tile_moe_shf_mlp_relu_kernel(
 
         nc.scalar.activation(ident[:], ident_raw[:], RELU)
 
+        nc.sync.dma_start(out=gate_cols[:], in_=gate[:, 0, :].rearrange("r (p c) -> p r c", p=P))
         load_tokens(0)
         nc.sync.dma_start(offs_sb[:], offs)
         for q in range(4):
@@ -146,13 +148,16 @@ def tile_moe_shf_mlp_relu_kernel(
         for j, (lo, hi) in enumerate(W2_PARTS):
             nc.sync.dma_start(out=w2[j][:].bitcast(I32),
                               in_=w2_words[lo:hi].bitcast(I32).rearrange("e s p c -> p (e s) c"))
-        for r, pos in enumerate((pos1, pos2, pos3)):
-            nc.sync.dma_start(pos_sb[r][:], pos)
-        nc.sync.dma_start(out=gates[0][:], in_=gate[0])
         nc.sync.dma_start(out=w2s[:], in_=w2s_words[0].rearrange("p n d -> p (n d)").bitcast(I32))
         load_scale_rows(nc, w2ssc[:], w2s_scales)
-        for r in range(1, TOP):
-            nc.sync.dma_start(out=gates[r][:], in_=gate[r])
+        for r, pos in enumerate((pos1, pos2, pos3)):
+            nc.sync.dma_start(pos_sb[r][:], pos)
+
+        for r in range(TOP):
+            spread = banks[r][:].rearrange("n (c p) -> n c p", p=P)
+            for c in range(T // P):
+                nc.tensor.transpose(spread[:, c, :], gate_cols[:, r, c:c + 1].to_broadcast([P, P]), ident[:])
+            nc.scalar.copy(gates[r][:].rearrange("n (p c) -> n p c", p=P), spread.rearrange("n c p -> n p c"))
 
         for e in range(0, E, 2):
             gather_words(e, e + 2)
@@ -162,6 +167,8 @@ def tile_moe_shf_mlp_relu_kernel(
         quantised = {}
 
         def first_bank(u):
+            if u < BLOCKS:
+                return banks[u % TOP]
             return banks[(2, 5, 7)[u // RUN % 3] if u % RUN == 2 else u % RUN]
 
         def turn_bank(i):
@@ -256,14 +263,18 @@ def tile_moe_shf_mlp_relu_kernel(
         terms = [sb("term%d" % r, [P, T], F32) for r in range(TOP)]
         sums = [sb("sum%d" % r, [P, T], F32) for r in range(TOP)]
         halves = [slice(0, T // 2), slice(T // 2, T)]
-        nc.vector.tensor_tensor(terms[0][:], y_slots[:].indirect(pos_sb[0][:]), gates[0][:], MULT)
+        entries = [slice(0, T // 32), slice(T // 32, T // 16)]
+        for cols, at in zip(halves, entries):
+            nc.vector.tensor_tensor(terms[0][:, cols], y_slots[:].indirect(pos_sb[0][:, at]), gates[0][:, cols], MULT)
         for r in range(1, TOP):
-            nc.scalar.activation(picked[r - 1][:], y_slots[:].indirect(pos_sb[r][:]), COPY)
-        nc.vector.tensor_tensor(terms[1][:], picked[0][:], gates[1][:], MULT)
-        nc.vector.tensor_tensor(sums[0][:], terms[0][:], shared[:], ADD)
-        nc.vector.tensor_tensor(terms[2][:], picked[1][:], gates[2][:], MULT)
+            for cols, at in zip(halves, entries):
+                nc.scalar.activation(picked[r - 1][:, cols], y_slots[:].indirect(pos_sb[r][:, at]), COPY)
         for cols in halves:
-            nc.vector.tensor_tensor(sums[1][:, cols], sums[0][:, cols], terms[1][:, cols], ADD)
+            nc.vector.tensor_tensor(sums[0][:, cols], terms[0][:, cols], shared[:, cols], ADD)
+        for r in range(1, TOP):
+            for cols in halves:
+                nc.vector.tensor_tensor(terms[r][:, cols], picked[r - 1][:, cols], gates[r][:, cols], MULT)
+            for cols in halves:
+                nc.vector.tensor_tensor(sums[r][:, cols], sums[r - 1][:, cols], terms[r][:, cols], ADD)
         for cols in halves:
-            nc.vector.tensor_tensor(sums[2][:, cols], sums[1][:, cols], terms[2][:, cols], ADD)
-            nc.sync.dma_start(out=out[:, cols], in_=sums[2][:, cols])
+            nc.sync.dma_start(out=out[:, cols], in_=sums[TOP - 1][:, cols])

@@ -26,13 +26,18 @@ ADD = mybir.AluOpType.add
 BLOCKS = T // C
 UNITS = BLOCKS + E
 RUN = 4
-GROUPS = [(e, e + 2) for e in range(0, E - 2, 2)] + [(E - 2, E - 1), (E - 1, E)]
-TURNS = [[u for u in turn if u >= 0] for lo in range(0, UNITS, RUN) for turn in ((lo + 2, lo - 1), (lo, lo + 1))]
-TURNS = TURNS + [[UNITS - 1]]
-VECTOR_TURNS = (1, 3, 5, 6)
+GROUPS = [(e, e + 2) for e in range(0, E - RUN, 2)] + [(e, e + 1) for e in range(E - RUN, E)]
+ALONE = (UNITS - RUN - 1, UNITS - 1)
+TURNS = [
+    turn
+    for lo in range(0, UNITS, RUN)
+    for turn in ([lo + 2] + [u for u in [lo - 1] if u >= 0 and u not in ALONE], [lo, lo + 1],
+                 [u for u in [lo + 3] if u in ALONE])
+    if turn
+]
+TURNS = TURNS[:-3] + [TURNS[-2], TURNS[-3], TURNS[-1]]
 BYTE_GATHER = 384
-BYTE_PARTS = [(0, RUN), (RUN, E)]
-W2_PARTS = [(0, 8), (8, E)]
+W2_PARTS = [(0, 4), (4, 8), (8, E - 1), (E - 1, E)]
 ZERO_WORDS = 32
 
 
@@ -74,8 +79,7 @@ def tile_moe_shf_mlp_relu_kernel(
         ident = sb("ident", [P, P], F32)
         y_slots = sb("y_slots", [P, SLOTS], F32)
         slot_words = [sb("slot_words%d" % s, [P, SLOTS], U32) for s in range(PASSES)]
-        slot_scales = [[sb("slot_scales%d_%d" % (lo, s), [P, (hi - lo) * C], U8) for s in range(PASSES)]
-                       for lo, hi in BYTE_PARTS]
+        slot_scales = [sb("slot_scales%d" % s, [P, SLOTS], U8) for s in range(PASSES)]
         banks = [psum.tile([P, H], F32, name="bank%d" % b) for b in range(8)]
 
         make_identity(nc, ident_raw[:])
@@ -85,8 +89,7 @@ def tile_moe_shf_mlp_relu_kernel(
         for plane in [w1ssc] + w1sc + [w2sc, w2ssc]:
             words = plane[:].bitcast(I32).rearrange("p (a b) -> p a b", b=ZERO_WORDS)
             nc.vector.tensor_copy(words, zero[:].unsqueeze(1).to_broadcast(list(words.shape)))
-        for both, lifted in slot_scales:
-            nc.vector.memset(lifted[:].bitcast(I32), 0)
+        nc.vector.memset(slot_scales[1][:].bitcast(I32), 0)
 
         def load_pass(dst, words, s):
             nc.sync.dma_start(out=dst, in_=words[s].rearrange("p t d -> p (t d)").bitcast(I32))
@@ -104,16 +107,15 @@ def tile_moe_shf_mlp_relu_kernel(
         def load_w1_scales(j):
             load_scale_rows(nc, w1sc[j][:], w1_scales[j * RUN:(j + 1) * RUN].rearrange("e s b i -> (e s) b i"))
 
-        def gather_scales(j):
-            lo, hi = BYTE_PARTS[j]
-            for at in range(0, (hi - lo) * C, BYTE_GATHER):
-                end = min(at + BYTE_GATHER, (hi - lo) * C)
-                entries = offs_sb[:, (lo * C + at) // 16:(lo * C + end) // 16]
-                nc.vector.tensor_copy(slot_scales[j][0][:, at:end], xs[:].indirect(entries))
+        def gather_scales():
+            for at in range(0, SLOTS, BYTE_GATHER):
+                entries = offs_sb[:, at // 16:(at + BYTE_GATHER) // 16]
+                nc.vector.tensor_copy(slot_scales[0][:, at:at + BYTE_GATHER], xs[:].indirect(entries))
 
-        def lift_scales(j):
-            both, lifted = slot_scales[j]
-            nc.sync.dma_start(out=lifted[0:P - 16, :].bitcast(I32), in_=both[4:P - 12, :].bitcast(I32))
+        def lift_scales():
+            for r in range(4):
+                nc.sync.dma_start(out=slot_scales[1][r:P:32, :].bitcast(I32),
+                                  in_=slot_scales[0][4 + r:P:32, :].bitcast(I32))
 
         def gather_words(lo, hi):
             entries = offs_sb[:, lo * C // 16:hi * C // 16]
@@ -131,14 +133,12 @@ def tile_moe_shf_mlp_relu_kernel(
         load_pass(w1s[1][:].bitcast(I32), w1s_words, 1)
         load_scale_rows(nc, w1ssc[:], w1s_scales)
         load_tokens(1)
-        gather_scales(0)
-        gather_scales(1)
+        gather_scales()
         load_w1_scales(0)
         load_w1_words(0)
-        lift_scales(0)
+        lift_scales()
         load_w1_words(1)
         load_w1_scales(1)
-        lift_scales(1)
         load_w1_words(2)
         load_w1_words(3)
         load_w1_scales(2)
@@ -171,10 +171,11 @@ def tile_moe_shf_mlp_relu_kernel(
                 return banks[u % TOP]
             return banks[(2, 5, 7)[u // RUN % 3] if u % RUN == 2 else u % RUN]
 
-        def turn_bank(i):
-            if i == len(TURNS) - 1:
-                return banks[5]
-            return first_bank(i // 2 * RUN + 2) if i % 2 else banks[4 + 2 * (i // 2 % 2)]
+        def turn_bank(turn):
+            if turn[0] % RUN == 0:
+                return first_bank(turn[0] + 2)
+            others = [t for t in TURNS if t[0] % RUN]
+            return banks[4 + 2 * (others.index(turn) % 2)]
 
         def relu_out(u):
             nc.scalar.activation(
@@ -191,13 +192,11 @@ def tile_moe_shf_mlp_relu_kernel(
 
         def first_layer(e):
             g = max(g for g, (lo, hi) in enumerate(GROUPS) if lo <= e)
-            j = max(j for j, (lo, hi) in enumerate(BYTE_PARTS) if lo <= e)
-            at = (e - BYTE_PARTS[j][0]) * C
             for s in range(PASSES):
                 plane_at = ((e % RUN) * PASSES + s) * H
                 nc.tensor.matmul_mx(
                     out=first_bank(BLOCKS + e)[:], lhsT=slot_words[s][:, e * C:(e + 1) * C].bitcast(FP8X4),
-                    lhsT_scale=slot_scales[j][s][:, at:at + C],
+                    lhsT_scale=slot_scales[s][:, e * C:(e + 1) * C],
                     rhs=w1[g][:, (e - GROUPS[g][0]) * PASSES + s, :].bitcast(FP4X4),
                     rhs_scale=w1sc[e // RUN][:, plane_at:plane_at + H],
                     start=(s == 0), stop=(s == PASSES - 1))
@@ -205,13 +204,13 @@ def tile_moe_shf_mlp_relu_kernel(
 
         def turn(i):
             n = len(TURNS[i])
-            view = turn_bank(i)[:].rearrange("p (u v j) -> p u v j", u=2, v=2)
+            view = turn_bank(TURNS[i])[:].rearrange("p (u v j) -> p u v j", u=2, v=2)
             for k, u in enumerate(TURNS[i]):
                 pairs = hidden[u].bitcast(F32)
                 for v in range(2):
                     nc.tensor.transpose(view[:, k, v, :], pairs[:, v * P:(v + 1) * P], ident[:])
             grouped[i] = sb("ht%d" % i, [P, n * C * 4], BF16)
-            copy = nc.vector.tensor_copy if i in VECTOR_TURNS else nc.scalar.copy
+            copy = nc.vector.tensor_copy if TURNS[i][0] % RUN == 0 else nc.scalar.copy
             copy(grouped[i][:].bitcast(F32).rearrange("p (u j v) -> p u j v", u=n, v=2),
                  view[:, 0:n].rearrange("p u v j -> p u j v"))
 
@@ -237,19 +236,17 @@ def tile_moe_shf_mlp_relu_kernel(
             for s in range(PASSES):
                 shared_pass(b, s)
             relu_out(b)
-        turn(0)
-        turn(1)
-        for lo in range(0, E, RUN):
-            for e in range(lo, lo + RUN):
+        for lo in range(0, UNITS, RUN):
+            for e in range(max(lo - BLOCKS, 0), lo - BLOCKS + RUN):
                 first_layer(e)
-            turn((BLOCKS + lo) // 2)
-            turn((BLOCKS + lo) // 2 + 1)
-        turn(len(TURNS) - 1)
+            for i in range(len(TURNS)):
+                if TURNS[i][0] // RUN == lo // RUN:
+                    turn(i)
         for i in range(len(TURNS)):
             quantise(i)
         second_layer(0, 4, banks[0], nc.scalar.copy)
         second_layer(4, 8, banks[1], nc.vector.tensor_copy)
-        second_layer(8, E - 1, banks[4], nc.scalar.copy)
+        second_layer(8, E - 1, banks[5], nc.scalar.copy)
         second_layer(E - 1, E, banks[3], nc.vector.tensor_copy)
 
         shared = banks[7]

@@ -27,15 +27,12 @@ BLOCKS = T // C
 UNITS = BLOCKS + E
 RUN = 4
 GROUPS = [(e, e + 2) for e in range(0, E - RUN, 2)] + [(e, e + 1) for e in range(E - RUN, E)]
-ALONE = (UNITS - RUN - 1, UNITS - 1)
-TURNS = [
-    turn
-    for lo in range(0, UNITS, RUN)
-    for turn in ([lo + 2] + [u for u in [lo - 1] if u >= 0 and u not in ALONE], [lo, lo + 1],
-                 [u for u in [lo + 3] if u in ALONE])
-    if turn
-]
-TURNS = TURNS[:-3] + [TURNS[-2], TURNS[-3], TURNS[-1]]
+FIRST_BANK = [0, 1, 2, 0, 3, 4, 5, 1, 0, 2, 3, 1, 0, 4, 5, 1]
+TURNS = {
+    7: [((5, 4), 6, False), ((0, 1), 4, False), ((6, 3), 7, True), ((2,), 5, True)],
+    11: [((10, 7), 6, False), ((8, 9), 3, True), ((11,), 2, False)],
+    15: [((12, 13), 5, True), ((14,), 6, False), ((15,), 7, False)],
+}
 BYTE_GATHER = 384
 W2_PARTS = [(0, 4), (4, 8), (8, E - 1), (E - 1, E)]
 ZERO_WORDS = 32
@@ -166,26 +163,15 @@ def tile_moe_shf_mlp_relu_kernel(
         grouped = {}
         quantised = {}
 
-        def first_bank(u):
-            if u < BLOCKS:
-                return banks[u % TOP]
-            return banks[(2, 5, 7)[u // RUN % 3] if u % RUN == 2 else u % RUN]
-
-        def turn_bank(turn):
-            if turn[0] % RUN == 0:
-                return first_bank(turn[0] + 2)
-            others = [t for t in TURNS if t[0] % RUN]
-            return banks[4 + 2 * (others.index(turn) % 2)]
-
         def relu_out(u):
             nc.scalar.activation(
                 hidden[u].rearrange("p (v m d) -> p v m d", v=2, d=2),
-                first_bank(u)[:].rearrange("p (m v d) -> p v m d", v=2, d=2), RELU)
+                banks[FIRST_BANK[u]][:].rearrange("p (m v d) -> p v m d", v=2, d=2), RELU)
 
         def shared_pass(b, s):
             t0 = b * C
             nc.tensor.matmul_mx(
-                out=first_bank(b)[:], lhsT=xw[:, s * T + t0:s * T + t0 + C].bitcast(FP8X4),
+                out=banks[FIRST_BANK[b]][:], lhsT=xw[:, s * T + t0:s * T + t0 + C].bitcast(FP8X4),
                 lhsT_scale=xs[4 * s:P, t0:t0 + C],
                 rhs=w1s[s][:].bitcast(FP8X4), rhs_scale=w1ssc[:, s * H:(s + 1) * H],
                 start=(s == 0), stop=(s == PASSES - 1))
@@ -195,30 +181,30 @@ def tile_moe_shf_mlp_relu_kernel(
             for s in range(PASSES):
                 plane_at = ((e % RUN) * PASSES + s) * H
                 nc.tensor.matmul_mx(
-                    out=first_bank(BLOCKS + e)[:], lhsT=slot_words[s][:, e * C:(e + 1) * C].bitcast(FP8X4),
+                    out=banks[FIRST_BANK[BLOCKS + e]][:], lhsT=slot_words[s][:, e * C:(e + 1) * C].bitcast(FP8X4),
                     lhsT_scale=slot_scales[s][:, e * C:(e + 1) * C],
                     rhs=w1[g][:, (e - GROUPS[g][0]) * PASSES + s, :].bitcast(FP4X4),
                     rhs_scale=w1sc[e // RUN][:, plane_at:plane_at + H],
                     start=(s == 0), stop=(s == PASSES - 1))
             relu_out(BLOCKS + e)
 
-        def turn(i):
-            n = len(TURNS[i])
-            view = turn_bank(TURNS[i])[:].rearrange("p (u v j) -> p u v j", u=2, v=2)
-            for k, u in enumerate(TURNS[i]):
+        def turn(units, bank, on_vector):
+            n = len(units)
+            view = banks[bank][:].rearrange("p (u v j) -> p u v j", u=2, v=2)
+            for k, u in enumerate(units):
                 pairs = hidden[u].bitcast(F32)
                 for v in range(2):
                     nc.tensor.transpose(view[:, k, v, :], pairs[:, v * P:(v + 1) * P], ident[:])
-            grouped[i] = sb("ht%d" % i, [P, n * C * 4], BF16)
-            copy = nc.vector.tensor_copy if TURNS[i][0] % RUN == 0 else nc.scalar.copy
-            copy(grouped[i][:].bitcast(F32).rearrange("p (u j v) -> p u j v", u=n, v=2),
+            grouped[units] = sb("ht%d" % units[0], [P, n * C * 4], BF16)
+            copy = nc.vector.tensor_copy if on_vector else nc.scalar.copy
+            copy(grouped[units][:].bitcast(F32).rearrange("p (u j v) -> p u j v", u=n, v=2),
                  view[:, 0:n].rearrange("p u v j -> p u j v"))
 
-        def quantise(i):
-            codes = sb("hq%d" % i, [P, len(TURNS[i]) * C], U32)
-            scales = sb("hsc%d" % i, [P, len(TURNS[i]) * C], U8)
-            nc.vector.quantize_mx(out=codes[:].bitcast(FP8X4), scales=scales[:], in_=grouped[i][:])
-            for k, u in enumerate(TURNS[i]):
+        def quantise(units):
+            codes = sb("hq%d" % units[0], [P, len(units) * C], U32)
+            scales = sb("hsc%d" % units[0], [P, len(units) * C], U8)
+            nc.vector.quantize_mx(out=codes[:].bitcast(FP8X4), scales=scales[:], in_=grouped[units][:])
+            for k, u in enumerate(units):
                 cols = slice(k * C, (k + 1) * C)
                 quantised[u] = (codes[:, cols].bitcast(FP8X4), scales[:, cols])
 
@@ -236,20 +222,18 @@ def tile_moe_shf_mlp_relu_kernel(
             for s in range(PASSES):
                 shared_pass(b, s)
             relu_out(b)
-        for lo in range(0, UNITS, RUN):
-            for e in range(max(lo - BLOCKS, 0), lo - BLOCKS + RUN):
-                first_layer(e)
-            for i in range(len(TURNS)):
-                if TURNS[i][0] // RUN == lo // RUN:
-                    turn(i)
-        for i in range(len(TURNS)):
-            quantise(i)
+        for e in range(E):
+            first_layer(e)
+            for units, bank, on_vector in TURNS.get(BLOCKS + e, []):
+                turn(units, bank, on_vector)
+        for units in grouped:
+            quantise(units)
         second_layer(0, 4, banks[0], nc.scalar.copy)
-        second_layer(4, 8, banks[1], nc.vector.tensor_copy)
-        second_layer(8, E - 1, banks[5], nc.scalar.copy)
-        second_layer(E - 1, E, banks[3], nc.vector.tensor_copy)
+        second_layer(4, 8, banks[4], nc.vector.tensor_copy)
+        second_layer(8, E - 1, banks[2], nc.scalar.copy)
+        second_layer(E - 1, E, banks[1], nc.vector.tensor_copy)
 
-        shared = banks[7]
+        shared = banks[3]
         for b in range(BLOCKS):
             codes, scales = quantised[b]
             nc.tensor.matmul_mx(

@@ -63,7 +63,7 @@ def tile_moe_shf_mlp_relu_kernel(
         xw = sb("xw", [P, PASSES * T], I32)
         xs = sb("xs", [P, T], U8)
         w1 = [sb("w1_%d" % lo, [P, (hi - lo) * PASSES, 2 * H], U8) for lo, hi in GROUPS]
-        w1s = [sb("w1s%d" % s, [P, H * 4], U8) for s in range(PASSES)]
+        w1s = sb("w1s", [P, PASSES, H * 4], U8)
         w1ssc = sb("w1ssc", [P, PASSES * H], U8)
         w1sc = [sb("w1sc_%d" % j, [P, RUN * PASSES * H], U8) for j in range(E // RUN)]
         w2sc = sb("w2sc", [P, E * N], U8)
@@ -88,13 +88,8 @@ def tile_moe_shf_mlp_relu_kernel(
             nc.vector.tensor_copy(words, zero[:].unsqueeze(1).to_broadcast(list(words.shape)))
         nc.vector.memset(slot_scales[1][:].bitcast(I32), 0)
 
-        def load_pass(dst, words, s):
-            nc.sync.dma_start(out=dst, in_=words[s].rearrange("p t d -> p (t d)").bitcast(I32))
-
-        def load_tokens(half):
-            cols = slice(half * T // 2, (half + 1) * T // 2)
-            nc.sync.dma_start(out=xw[:].rearrange("p (s t) -> p s t", s=PASSES)[:, :, cols],
-                              in_=x_words[:, :, cols, :].rearrange("s p t d -> p s (t d)").bitcast(I32))
+        def load_tokens(s):
+            nc.sync.dma_start(out=xw[:, s * T:(s + 1) * T], in_=x_words[s].rearrange("p t d -> p (t d)").bitcast(I32))
 
         def load_w1_words(g):
             lo, hi = GROUPS[g]
@@ -103,6 +98,11 @@ def tile_moe_shf_mlp_relu_kernel(
 
         def load_w1_scales(j):
             load_scale_rows(nc, w1sc[j][:], w1_scales[j * RUN:(j + 1) * RUN].rearrange("e s b i -> (e s) b i"))
+
+        def load_w2_words(j):
+            lo, hi = W2_PARTS[j]
+            nc.sync.dma_start(out=w2[j][:].bitcast(I32),
+                              in_=w2_words[lo:hi].bitcast(I32).rearrange("e s p c -> p (e s) c"))
 
         def gather_scales():
             for at in range(0, SLOTS, BYTE_GATHER):
@@ -126,29 +126,28 @@ def tile_moe_shf_mlp_relu_kernel(
         nc.sync.dma_start(offs_sb[:], offs)
         for q in range(4):
             nc.sync.dma_start(out=xs[32 * q:32 * q + 8, :].bitcast(I32), in_=x_scales[:, 4 * q:4 * q + 4, :].bitcast(I32))
-        load_pass(w1s[0][:].bitcast(I32), w1s_words, 0)
-        load_pass(w1s[1][:].bitcast(I32), w1s_words, 1)
-        load_scale_rows(nc, w1ssc[:], w1s_scales)
+        nc.sync.dma_start(out=w1s[:].bitcast(I32), in_=w1s_words.rearrange("s p l d -> p s (l d)").bitcast(I32))
         load_tokens(1)
+        load_scale_rows(nc, w1ssc[:], w1s_scales)
         gather_scales()
-        load_w1_scales(0)
         load_w1_words(0)
-        lift_scales()
+        load_w1_scales(0)
         load_w1_words(1)
-        load_w1_scales(1)
+        lift_scales()
         load_w1_words(2)
+        load_w1_scales(1)
         load_w1_words(3)
         load_w1_scales(2)
         for g in range(4, len(GROUPS)):
             load_w1_words(g)
         load_scale_rows(nc, w2sc[:], w2_scales.rearrange("e s b n -> (e s) b n"))
-        for j, (lo, hi) in enumerate(W2_PARTS):
-            nc.sync.dma_start(out=w2[j][:].bitcast(I32),
-                              in_=w2_words[lo:hi].bitcast(I32).rearrange("e s p c -> p (e s) c"))
-        nc.sync.dma_start(out=w2s[:], in_=w2s_words[0].rearrange("p n d -> p (n d)").bitcast(I32))
-        load_scale_rows(nc, w2ssc[:], w2s_scales)
+        for j in range(len(W2_PARTS) - 1):
+            load_w2_words(j)
         for r, pos in enumerate((pos1, pos2, pos3)):
             nc.sync.dma_start(pos_sb[r][:], pos)
+        load_w2_words(len(W2_PARTS) - 1)
+        nc.sync.dma_start(out=w2s[:], in_=w2s_words[0].rearrange("p n d -> p (n d)").bitcast(I32))
+        load_scale_rows(nc, w2ssc[:], w2s_scales)
 
         for r in range(TOP):
             spread = banks[r][:].rearrange("n (c p) -> n c p", p=P)
@@ -173,19 +172,20 @@ def tile_moe_shf_mlp_relu_kernel(
             nc.tensor.matmul_mx(
                 out=banks[FIRST_BANK[b]][:], lhsT=xw[:, s * T + t0:s * T + t0 + C].bitcast(FP8X4),
                 lhsT_scale=xs[4 * s:P, t0:t0 + C],
-                rhs=w1s[s][:].bitcast(FP8X4), rhs_scale=w1ssc[:, s * H:(s + 1) * H],
+                rhs=w1s[:, s, :].bitcast(FP8X4), rhs_scale=w1ssc[:, s * H:(s + 1) * H],
                 start=(s == 0), stop=(s == PASSES - 1))
 
         def first_layer(e):
             g = max(g for g, (lo, hi) in enumerate(GROUPS) if lo <= e)
-            for s in range(PASSES):
+            order = list(reversed(range(PASSES))) if g == 1 else list(range(PASSES))
+            for s in order:
                 plane_at = ((e % RUN) * PASSES + s) * H
                 nc.tensor.matmul_mx(
                     out=banks[FIRST_BANK[BLOCKS + e]][:], lhsT=slot_words[s][:, e * C:(e + 1) * C].bitcast(FP8X4),
                     lhsT_scale=slot_scales[s][:, e * C:(e + 1) * C],
                     rhs=w1[g][:, (e - GROUPS[g][0]) * PASSES + s, :].bitcast(FP4X4),
                     rhs_scale=w1sc[e // RUN][:, plane_at:plane_at + H],
-                    start=(s == 0), stop=(s == PASSES - 1))
+                    start=(s == order[0]), stop=(s == order[-1]))
             relu_out(BLOCKS + e)
 
         def turn(units, bank, on_vector):
@@ -250,12 +250,12 @@ def tile_moe_shf_mlp_relu_kernel(
         for r in range(1, TOP):
             for cols, at in zip(halves, entries):
                 nc.scalar.activation(picked[r - 1][:, cols], y_slots[:].indirect(pos_sb[r][:, at]), COPY)
-        for cols in halves:
-            nc.vector.tensor_tensor(sums[0][:, cols], terms[0][:, cols], shared[:, cols], ADD)
         for r in range(1, TOP):
+            before = terms[0] if r == 1 else sums[r - 2]
             for cols in halves:
                 nc.vector.tensor_tensor(terms[r][:, cols], picked[r - 1][:, cols], gates[r][:, cols], MULT)
             for cols in halves:
-                nc.vector.tensor_tensor(sums[r][:, cols], sums[r - 1][:, cols], terms[r][:, cols], ADD)
+                nc.vector.tensor_tensor(sums[r - 1][:, cols], before[:, cols], terms[r][:, cols], ADD)
         for cols in halves:
+            nc.vector.tensor_tensor(sums[TOP - 1][:, cols], sums[TOP - 2][:, cols], shared[:, cols], ADD)
             nc.sync.dma_start(out=out[:, cols], in_=sums[TOP - 1][:, cols])

from contextlib import ExitStack

import concourse.mybir as mybir
from concourse.masks import make_identity

K, T, E, C, H, N = 1024, 512, 12, 128, 512, 128
TOP = 3
P = 128
PASSES = K // 512
SLOTS = E * C
FLOPS = 2 * (SLOTS + T) * (K * H + H * N)

F32 = mybir.dt.float32
BF16 = mybir.dt.bfloat16
I32 = mybir.dt.int32
U32 = mybir.dt.uint32
U16 = mybir.dt.uint16
U8 = mybir.dt.uint8
FP8X4 = mybir.dt.float8_e4m3fn_x4
FP4X4 = mybir.dt.float4_e2m1fn_x4
RELU = mybir.ActivationFunctionType.Relu
COPY = mybir.ActivationFunctionType.Copy
MULT = mybir.AluOpType.mult
ADD = mybir.AluOpType.add

BLOCKS = T // C
UNITS = BLOCKS + E
RUN = 4
GROUPS = [(e, e + 2) for e in range(0, E - RUN, 2)] + [(e, e + 1) for e in range(E - RUN, E)]
FIRST_BANK = [0, 1, 2, 0, 3, 4, 5, 1, 0, 2, 3, 1, 0, 4, 5, 1]
TURNS = {
    7: [((5, 4), 6, False), ((0, 1), 4, False), ((6, 3), 7, True), ((2,), 5, True)],
    11: [((10, 7), 6, False), ((8, 9), 3, True), ((11,), 2, False)],
    15: [((12, 13), 5, True), ((14,), 6, False), ((15,), 7, False)],
}
BYTE_GATHER = 384
W2_PARTS = [(0, 4), (4, 8), (8, E - 1), (E - 1, E)]
ZERO_WORDS = 32


def load_scale_rows(nc, plane, rows):
    sets = rows.shape[0]
    src = rows.bitcast(I32).rearrange("g (q r) w -> r q g w", r=4)
    dst = plane.bitcast(I32).rearrange("p (g w) -> p g w", g=sets)
    for r in range(4):
        nc.sync.dma_start(out=dst[r:P:32], in_=src[r])


def tile_moe_shf_mlp_relu_kernel(
    tc, x_words, x_scales, w1_words, w1_scales, w2_words, w2_scales, w1s_words, w1s_scales, w2s_words, w2s_scales,
    gate, offs, pos1, pos2, pos3, out,
):
    nc = tc.nc
    with ExitStack() as ctx:
        keep = ctx.enter_context(tc.tile_pool(name="keep", bufs=1))
        psum = ctx.enter_context(tc.psum_pool(name="psum", bufs=1))

        def sb(name, shape, dtype):
            return keep.tile(shape, dtype, name=name, align_bytes=256)

        offs_sb = keep.tile([P, SLOTS // 16], U16, name="offs_sb")
        pos_sb = [keep.tile([P, T // 16], U16, name="pos%d_sb" % r) for r in range(TOP)]
        xw = sb("xw", [P, PASSES * T], I32)
        xs = sb("xs", [P, T], U8)
        w1 = [sb("w1_%d" % lo, [P, (hi - lo) * PASSES, 2 * H], U8) for lo, hi in GROUPS]
        w1s = sb("w1s", [P, PASSES, H * 4], U8)
        w1ssc = sb("w1ssc", [P, PASSES * H], U8)
        w1sc = [sb("w1sc_%d" % j, [P, RUN * PASSES * H], U8) for j in range(E // RUN)]
        w2sc = sb("w2sc", [P, E * N], U8)
        w2ssc = sb("w2ssc", [P, N], U8)
        w2 = [sb("w2_%d" % lo, [P, hi - lo, 2 * N], U8) for lo, hi in W2_PARTS]
        w2s = sb("w2s", [P, N], I32)
        gate_cols = sb("gate_cols", [P, TOP, T // P], F32)
        gates = [sb("gate%d" % r, [P, T], F32) for r in range(TOP)]
        ident_raw = sb("ident_raw", [P, P], F32)
        ident = sb("ident", [P, P], F32)
        y_slots = sb("y_slots", [P, SLOTS], F32)
        slot_words = [sb("slot_words%d" % s, [P, SLOTS], U32) for s in range(PASSES)]
        slot_scales = [sb("slot_scales%d" % s, [P, SLOTS], U8) for s in range(PASSES)]
        banks = [psum.tile([P, H], F32, name="bank%d" % b) for b in range(8)]

        make_identity(nc, ident_raw[:])
        zero = sb("zero", [P, ZERO_WORDS], I32)
        nc.vector.memset(xs[:].bitcast(I32), 0)
        nc.vector.memset(zero[:], 0)
        for plane in [w1ssc] + w1sc + [w2sc, w2ssc]:
            words = plane[:].bitcast(I32).rearrange("p (a b) -> p a b", b=ZERO_WORDS)
            nc.vector.tensor_copy(words, zero[:].unsqueeze(1).to_broadcast(list(words.shape)))
        nc.vector.memset(slot_scales[1][:].bitcast(I32), 0)

        def load_tokens(s):
            nc.sync.dma_start(out=xw[:, s * T:(s + 1) * T], in_=x_words[s].rearrange("p t d -> p (t d)").bitcast(I32))

        def load_w1_words(g):
            lo, hi = GROUPS[g]
            src = w1_words[lo:hi].bitcast(I32).rearrange("e s p c -> p (e s) c")
            nc.sync.dma_start(out=w1[g][:].bitcast(I32), in_=src)

        def load_w1_scales(j):
            load_scale_rows(nc, w1sc[j][:], w1_scales[j * RUN:(j + 1) * RUN].rearrange("e s b i -> (e s) b i"))

        def load_w2_words(j):
            lo, hi = W2_PARTS[j]
            nc.sync.dma_start(out=w2[j][:].bitcast(I32),
                              in_=w2_words[lo:hi].bitcast(I32).rearrange("e s p c -> p (e s) c"))

        def gather_scales():
            for at in range(0, SLOTS, BYTE_GATHER):
                entries = offs_sb[:, at // 16:(at + BYTE_GATHER) // 16]
                nc.vector.tensor_copy(slot_scales[0][:, at:at + BYTE_GATHER], xs[:].indirect(entries))

        def lift_scales():
            for r in range(4):
                nc.sync.dma_start(out=slot_scales[1][r:P:32, :].bitcast(I32),
                                  in_=slot_scales[0][4 + r:P:32, :].bitcast(I32))

        def gather_words(lo, hi):
            entries = offs_sb[:, lo * C // 16:hi * C // 16]
            for s in range(PASSES):
                nc.vector.tensor_copy(slot_words[s][:, lo * C:hi * C], xw[:, s * T:].bitcast(U32).indirect(entries))

        nc.scalar.activation(ident[:], ident_raw[:], RELU)

        nc.sync.dma_start(out=gate_cols[:], in_=gate[:, 0, :].rearrange("r (p c) -> p r c", p=P))
        load_tokens(0)
        nc.sync.dma_start(offs_sb[:], offs)
        for q in range(4):
            nc.sync.dma_start(out=xs[32 * q:32 * q + 8, :].bitcast(I32), in_=x_scales[:, 4 * q:4 * q + 4, :].bitcast(I32))
        nc.sync.dma_start(out=w1s[:].bitcast(I32), in_=w1s_words.rearrange("s p l d -> p s (l d)").bitcast(I32))
        load_tokens(1)
        load_scale_rows(nc, w1ssc[:], w1s_scales)
        gather_scales()
        load_w1_words(0)
        load_w1_scales(0)
        load_w1_words(1)
        lift_scales()
        load_w1_words(2)
        load_w1_scales(1)
        load_w1_words(3)
        load_w1_scales(2)
        for g in range(4, len(GROUPS)):
            load_w1_words(g)
        load_scale_rows(nc, w2sc[:], w2_scales.rearrange("e s b n -> (e s) b n"))
        for j in range(len(W2_PARTS) - 1):
            load_w2_words(j)
        for r, pos in enumerate((pos1, pos2, pos3)):
            nc.sync.dma_start(pos_sb[r][:], pos)
        load_w2_words(len(W2_PARTS) - 1)
        nc.sync.dma_start(out=w2s[:], in_=w2s_words[0].rearrange("p n d -> p (n d)").bitcast(I32))
        load_scale_rows(nc, w2ssc[:], w2s_scales)

        for r in range(TOP):
            spread = banks[r][:].rearrange("n (c p) -> n c p", p=P)
            for c in range(T // P):
                nc.tensor.transpose(spread[:, c, :], gate_cols[:, r, c:c + 1].to_broadcast([P, P]), ident[:])
            nc.scalar.copy(gates[r][:].rearrange("n (p c) -> n p c", p=P), spread.rearrange("n c p -> n p c"))

        for e in range(0, E, 2):
            gather_words(e, e + 2)

        hidden = [sb("h%d" % u, [P, H], BF16)[:] for u in range(UNITS)]
        grouped = {}
        quantised = {}

        def relu_out(u):
            nc.scalar.activation(
                hidden[u].rearrange("p (v m d) -> p v m d", v=2, d=2),
                banks[FIRST_BANK[u]][:].rearrange("p (m v d) -> p v m d", v=2, d=2), RELU)

        def shared_pass(b, s):
            t0 = b * C
            nc.tensor.matmul_mx(
                out=banks[FIRST_BANK[b]][:], lhsT=xw[:, s * T + t0:s * T + t0 + C].bitcast(FP8X4),
                lhsT_scale=xs[4 * s:P, t0:t0 + C],
                rhs=w1s[:, s, :].bitcast(FP8X4), rhs_scale=w1ssc[:, s * H:(s + 1) * H],
                start=(s == 0), stop=(s == PASSES - 1))

        def first_layer(e):
            g = max(g for g, (lo, hi) in enumerate(GROUPS) if lo <= e)
            order = list(reversed(range(PASSES))) if g == 1 else list(range(PASSES))
            for s in order:
                plane_at = ((e % RUN) * PASSES + s) * H
                nc.tensor.matmul_mx(
                    out=banks[FIRST_BANK[BLOCKS + e]][:], lhsT=slot_words[s][:, e * C:(e + 1) * C].bitcast(FP8X4),
                    lhsT_scale=slot_scales[s][:, e * C:(e + 1) * C],
                    rhs=w1[g][:, (e - GROUPS[g][0]) * PASSES + s, :].bitcast(FP4X4),
                    rhs_scale=w1sc[e // RUN][:, plane_at:plane_at + H],
                    start=(s == order[0]), stop=(s == order[-1]))
            relu_out(BLOCKS + e)

        def turn(units, bank, on_vector):
            n = len(units)
            view = banks[bank][:].rearrange("p (u v j) -> p u v j", u=2, v=2)
            for k, u in enumerate(units):
                pairs = hidden[u].bitcast(F32)
                for v in range(2):
                    nc.tensor.transpose(view[:, k, v, :], pairs[:, v * P:(v + 1) * P], ident[:])
            grouped[units] = sb("ht%d" % units[0], [P, n * C * 4], BF16)
            copy = nc.vector.tensor_copy if on_vector else nc.scalar.copy
            copy(grouped[units][:].bitcast(F32).rearrange("p (u j v) -> p u j v", u=n, v=2),
                 view[:, 0:n].rearrange("p u v j -> p u j v"))

        def quantise(units):
            codes = sb("hq%d" % units[0], [P, len(units) * C], U32)
            scales = sb("hsc%d" % units[0], [P, len(units) * C], U8)
            nc.vector.quantize_mx(out=codes[:].bitcast(FP8X4), scales=scales[:], in_=grouped[units][:])
            for k, u in enumerate(units):
                cols = slice(k * C, (k + 1) * C)
                quantised[u] = (codes[:, cols].bitcast(FP8X4), scales[:, cols])

        def second_layer(first, end, bank, copy):
            for e in range(first, end):
                codes, scales = quantised[BLOCKS + e]
                part = max(j for j, (lo, hi) in enumerate(W2_PARTS) if lo <= e)
                nc.tensor.matmul_mx(
                    out=bank[:, (e - first) * C:(e - first + 1) * C],
                    lhsT=w2[part][:, e - W2_PARTS[part][0], :].bitcast(FP4X4), lhsT_scale=w2sc[:, e * N:(e + 1) * N],
                    rhs=codes, rhs_scale=scales, start=True, stop=True)
            copy(y_slots[:, first * C:end * C], bank[:, 0:(end - first) * C])

        for b in range(BLOCKS):
            for s in range(PASSES):
                shared_pass(b, s)
            relu_out(b)
        for e in range(E):
            first_layer(e)
            for units, bank, on_vector in TURNS.get(BLOCKS + e, []):
                turn(units, bank, on_vector)
        for units in grouped:
            quantise(units)
        second_layer(0, 4, banks[0], nc.scalar.copy)
        second_layer(4, 8, banks[4], nc.vector.tensor_copy)
        second_layer(8, E - 1, banks[2], nc.scalar.copy)
        second_layer(E - 1, E, banks[1], nc.vector.tensor_copy)

        shared = banks[3]
        for b in range(BLOCKS):
            codes, scales = quantised[b]
            nc.tensor.matmul_mx(
                out=shared[:, b * C:(b + 1) * C], lhsT=w2s[:].bitcast(FP8X4), lhsT_scale=w2ssc[:],
                rhs=codes, rhs_scale=scales, start=True, stop=True)

        picked = [sb("picked%d" % r, [P, T], F32) for r in range(1, TOP)]
        terms = [sb("term%d" % r, [P, T], F32) for r in range(TOP)]
        sums = [sb("sum%d" % r, [P, T], F32) for r in range(TOP)]
        halves = [slice(0, T // 2), slice(T // 2, T)]
        entries = [slice(0, T // 32), slice(T // 32, T // 16)]
        for cols, at in zip(halves, entries):
            nc.vector.tensor_tensor(terms[0][:, cols], y_slots[:].indirect(pos_sb[0][:, at]), gates[0][:, cols], MULT)
        for r in range(1, TOP):
            for cols, at in zip(halves, entries):
                nc.scalar.activation(picked[r - 1][:, cols], y_slots[:].indirect(pos_sb[r][:, at]), COPY)
        for r in range(1, TOP):
            before = terms[0] if r == 1 else sums[r - 2]
            for cols in halves:
                nc.vector.tensor_tensor(terms[r][:, cols], picked[r - 1][:, cols], gates[r][:, cols], MULT)
            for cols in halves:
                nc.vector.tensor_tensor(sums[r - 1][:, cols], before[:, cols], terms[r][:, cols], ADD)
        for cols in halves:
            nc.vector.tensor_tensor(sums[TOP - 1][:, cols], sums[TOP - 2][:, cols], shared[:, cols], ADD)
            nc.sync.dma_start(out=out[:, cols], in_=sums[TOP - 1][:, cols])
